import numpy as np
import ml_dtypes


def mxq(x, axis, fmt="e4m3"):
    dtype, down = {"e4m3": (ml_dtypes.float8_e4m3fn, 7), "e5m2": (ml_dtypes.float8_e5m2, 14)}[fmt]
    v = np.moveaxis(np.asarray(x, np.float32).astype(ml_dtypes.bfloat16).astype(np.float64), axis, -1)
    blocks = v.reshape(v.shape[:-1] + (-1, 32))
    amax = np.abs(blocks).max(-1, keepdims=True)
    byte = np.maximum(np.where(amax > 0, np.frexp(amax)[1] - 1 + 127, 0) - down, 1)
    scale = np.exp2(byte - 127.0)
    codes = (blocks / scale).astype(np.float32).astype(dtype).astype(np.float64)
    return np.moveaxis((codes * scale).reshape(v.shape), -1, axis)


WIDE = False


def mx_kscale(k):
    if not WIDE:
        return np.ones(k)
    levels = np.array([10, -10, 5, -5, 0])
    if k % 512:
        return np.exp2(np.random.permutation(np.resize(levels, k // 32))).repeat(32)
    a = np.empty((k // 512, 16))
    for p in range(k // 512):
        a[p, :8] = np.random.permutation(np.resize(levels, 8))
        for g in range(8):
            far = levels[np.abs(levels - a[p, g]) >= 10]
            a[p, g + 8] = far[np.random.randint(len(far))]
    return np.exp2(a.ravel()).repeat(32)


def f64(x):
    return np.asarray(x).astype(np.float64)


def striped(idx):
    return np.tile(np.asarray(idx).reshape(-1, 16).T, (8, 1)).astype(np.uint16)


def unstriped(offs):
    return offs[:16].T.reshape(-1).astype(np.int64)


E2M1 = np.array([0.0, 0.5, 1.0, 1.5, 2.0, 3.0, 4.0, 6.0, -0.0, -0.5, -1.0, -1.5, -2.0, -3.0, -4.0, -6.0])


def pack_weight(w, fmt):
    k, n = w.shape
    w = f64(np.asarray(w, np.float32).astype(ml_dtypes.bfloat16)).reshape(k // 32, 32, n)
    amax = np.abs(w).max(1)
    if fmt == "e4m3":
        byte = np.frexp(amax)[1] - 1 + 127 - 7
    else:
        mant, ex = np.frexp(amax / 6.0)
        byte = np.where(mant > 0.5, ex, ex - 1) + 127
    byte = np.clip(np.where(amax > 0, byte, 1), 1, 254)
    scaled = (w * np.exp2(127.0 - byte)[:, None, :]).reshape(k, n).astype(np.float32)
    by_word = np.ascontiguousarray(scaled.reshape(k // 512, 128, 4, n).transpose(0, 1, 3, 2))
    if fmt == "e4m3":
        words = by_word.astype(ml_dtypes.float8_e4m3fn).view(np.uint8)
    else:
        c = by_word.astype(ml_dtypes.float4_e2m1fn).view(np.uint8) & 0xF
        words = (c[..., 0::2] | (c[..., 1::2] << 4)).reshape(k // 512, 128, 2 * n)
    return np.ascontiguousarray(words), np.ascontiguousarray(byte.astype(np.uint8).reshape(k // 512, 16, n))


def unpack_weight(words, scales, fmt):
    g, _, n = scales.shape
    words = np.ascontiguousarray(words).reshape(g, 128, n, -1)
    if fmt == "e4m3":
        vals = words.view(ml_dtypes.float8_e4m3fn).astype(np.float64)
    else:
        nib = np.empty((g, 128, n, 4), np.uint8)
        nib[..., 0::2] = words & 0xF
        nib[..., 1::2] = words >> 4
        vals = E2M1[nib]
    vals = vals * np.repeat(np.exp2(scales.astype(np.float64) - 127.0), 8, axis=1)[..., None]
    return vals.transpose(0, 1, 3, 2).reshape(g * 512, n)


B, N, T, D, DV, NQ = 1, 1536, 4096, 512, 256, 256
PAGE = 512
CAP = 2.0
DRAFT = 128


def setup_inputs():
    n = np.random.standard_normal
    pages = np.random.permutation(T // PAGE)[:B * N // PAGE]
    idx = (pages[:, None] * PAGE + np.arange(PAGE)[None, :]).reshape(-1)
    s = mx_kscale(D)[:, None]
    u = np.ones(T)
    u[idx] = mx_kscale(B * N)
    r = np.random.uniform(0.5, 2.0, T)
    qp = [pack_weight(x, "e4m3") for x in n((B, D, NQ)) * s * (0.80 / np.sqrt(D))]
    k = n((D, T)) / s
    v = n((DV, T)) / (u * r)
    kp = pack_weight(k, "e4m3")
    vp = pack_weight(v.T, "e4m3")
    when = np.zeros(T)
    when[idx] = np.concatenate([np.concatenate([np.arange(N - DRAFT), N - DRAFT + np.random.randint(0, 16, DRAFT)]) for b in range(B)])
    return {
        "q_words": np.stack([x[0] for x in qp]),
        "q_scales": np.stack([x[1] for x in qp]),
        "k_words": kp[0],
        "k_scales": kp[1],
        "v_words": vp[0],
        "v_scales": vp[1],
        "vs": np.tile(u * r, (128, 1)).astype(np.float32),
        "pos": np.tile(when, (128, 1)).astype(np.float32),
        "qpos": np.random.randint(N - DRAFT, N - DRAFT + 16, (B, NQ, 1)).astype(np.float32),
        "offs": striped(idx),
        "voffs": striped((pages[:, None] * DV + np.arange(DV)[None, :]).reshape(-1)),
    }


def reference(q_words, q_scales, k_words, k_scales, v_words, v_scales, vs, pos, qpos, offs, voffs):
    idx = unstriped(offs)
    k = unpack_weight(k_words, k_scales, "e4m3")
    v = unpack_weight(v_words, v_scales, "e4m3")
    v = v.reshape(T // 512, 512, DV)[unstriped(voffs)[::DV] // DV].reshape(B, N, DV)
    pick = lambda x: x[:, idx].reshape(x.shape[0], B, N).transpose(1, 0, 2)
    q = np.stack([unpack_weight(q_words[b], q_scales[b], "e4m3") for b in range(B)])
    score = q.transpose(0, 2, 1) @ pick(k)
    score = CAP * np.tanh(score / CAP)
    score = np.where(pick(f64(pos))[:, :1, :] <= f64(qpos), score, -30000.0)
    m = score.max(-1, keepdims=True)
    p = np.exp(score - m)
    total = p.sum(-1, keepdims=True)
    w = p * pick(f64(vs))[:, :1, :]
    y = mxq(w, 2, "e4m3") @ v
    y = y / total
    return y

@@ -1,0 +1,275 @@
+from contextlib import ExitStack
+
+import concourse.mybir as mybir
+from concourse.masks import make_identity
+
+N, T, D, DV, NQ = 1536, 4096, 512, 256, 256
+PAGE = 512
+CAP = 2.0
+MASKED = -30000.0
+FLOPS = 2 * NQ * N * (D + DV)
+
+F32 = mybir.dt.float32
+BF16 = mybir.dt.bfloat16
+I32 = mybir.dt.int32
+U32 = mybir.dt.uint32
+U16 = mybir.dt.uint16
+U8 = mybir.dt.uint8
+FP8X4 = mybir.dt.float8_e4m3fn_x4
+ALU = mybir.AluOpType
+ACT = mybir.ActivationFunctionType
+AXIS = mybir.AxisListType
+
+P = 128
+PACK = 4
+PAGES = N // PAGE
+POOL_PAGES = T // PAGE
+BLOCKS = NQ // P
+LIST_COLS = PAGE // 16
+ROW = P - 1
+STEEP = 2.0**60
+
+
+def tile_attend_pkv8q_soft_draft_cap_kernel(
+    tc, q_words, q_scales, k_words, k_scales, v_words, v_scales, vs, pos, qpos, offs, voffs, out
+):
+    nc = tc.nc
+    with ExitStack() as ctx:
+        sb = ctx.enter_context(tc.tile_pool(name="sb", bufs=1))
+        psum = ctx.enter_context(tc.psum_pool(name="psum", bufs=1))
+
+        def bank(index, shape):
+            return psum.tile(shape, F32, name="bank%d" % index, tag="bank%d" % index)
+
+        def page_list(u):
+            return offs_t[:, u * LIST_COLS : (u + 1) * LIST_COLS]
+
+        offs_t = sb.tile([P, N // 16], U16, name="offs_t")
+        voffs_t = sb.tile([P, PAGES * DV // 16], U16, name="voffs_t")
+        pos_pool = sb.tile([P, T], F32, name="pos_pool")
+        vs_pool = sb.tile([P, T], F32, name="vs_pool")
+        kw_pool = sb.tile([P, T], I32, name="kw_pool")
+        ks_pool = sb.tile([P, T], U8, name="ks_pool")
+        vw_pool = sb.tile([P, POOL_PAGES * DV], I32, name="vw_pool")
+        vsc_pool = sb.tile([P, POOL_PAGES * DV], U8, name="vsc_pool")
+        qw = sb.tile([P, NQ], I32, name="qw", align_bytes=64)
+        qs = sb.tile([P, NQ], U8, name="qs", align_bytes=64)
+        qpos_cols = sb.tile([P, BLOCKS], F32, name="qpos_cols")
+        ident = sb.tile([P, P], F32, name="ident")
+        warm_in = sb.tile([P, 1], F32, name="warm_in")
+        warm_out = sb.tile([P, 1], F32, name="warm_out")
+
+        nc.vector.memset(ks_pool[:].bitcast(I32), 0)
+        nc.vector.memset(warm_in[:], 0.0)
+        nc.vector.memset(qs[:].bitcast(I32), 0)
+        nc.scalar.activation(warm_out[:], warm_in[:], ACT.Exp)
+        make_identity(nc, ident[:])
+
+        nc.sync.dma_start(offs_t[:], offs)
+        nc.sync.dma_start(pos_pool[ROW:P, :], pos[ROW:P, :])
+        nc.sync.dma_start(qpos_cols[:], qpos[0].rearrange("(p c) o -> p (c o)", c=BLOCKS))
+        k_scale_rows = k_scales[0].rearrange("(g r) t -> r g t", r=PACK)
+        for r in range(PACK):
+            nc.sync.dma_start(ks_pool[r:P:32, :].bitcast(I32), k_scale_rows[r].bitcast(I32))
+        nc.sync.dma_start(kw_pool[:], k_words[0].rearrange("p t r -> p (t r)").bitcast(I32))
+
+        nc.scalar.dma_start(qw[:], q_words[0, 0].rearrange("p q r -> p (q r)").bitcast(I32))
+        q_scale_rows = q_scales[0, 0].rearrange("(g r) q -> r g q", r=PACK)
+        for r in range(PACK):
+            nc.scalar.dma_start(qs[r:P:32, :].bitcast(I32), q_scale_rows[r].bitcast(I32))
+
+        nc.vector.memset(pos_pool[0:ROW, :], 0.0)
+        nc.vector.memset(vs_pool[0:ROW, 0:64], 0.0)
+        nc.gpsimd.memset(vs_pool[0:ROW, 56:T], 0.0)
+
+        qpos_bank = bank(6, [P, BLOCKS, P])
+        for c in range(BLOCKS):
+            nc.tensor.transpose(qpos_bank[:, c, :], qpos_cols[:, c : c + 1].to_broadcast([P, P]), ident[:])
+        qpos_rows = sb.tile([P, NQ], F32, name="qpos_rows")
+        nc.scalar.activation(
+            qpos_rows[:].rearrange("p (q c) -> p q c", c=BLOCKS), qpos_bank[:].rearrange("p c q -> p q c"), ACT.Copy
+        )
+
+        pos_g = sb.tile([P, N], F32, name="pos_g")
+        pos_cols = sb.tile([P, PAGES * PACK], F32, name="pos_cols")
+        late = sb.tile([P, PAGES * PACK, NQ], F32, name="late")
+        capped_banks = [[bank(b * PAGES + u, [P, PAGE]) for u in range(PAGES)] for b in range(BLOCKS)]
+        for u in range(PAGES):
+            nc.vector.tensor_copy(pos_g[:, u * PAGE : (u + 1) * PAGE], pos_pool[:].indirect(page_list(u)))
+            pos_bank = bank(7 - u % 2, [P, PACK, P])
+            for j in range(PACK):
+                first = u * PAGE + j * P
+                nc.tensor.transpose(pos_bank[:, j, :], pos_g[:, first : first + P], ident[:])
+            nc.scalar.activation(pos_cols[:, u * PACK : (u + 1) * PACK], pos_bank[:, :, ROW], ACT.Copy, scale=STEEP)
+            for j in range(PACK):
+                chunk = u * PACK + j
+                nc.scalar.activation(
+                    late[:, chunk, :], qpos_rows[:], ACT.Relu, bias=pos_cols[:, chunk : chunk + 1], scale=-STEEP
+                )
+            for b in range(BLOCKS):
+                for j in range(PACK):
+                    nc.tensor.matmul(
+                        capped_banks[b][u][:, j * P : (j + 1) * P],
+                        lhsT=late[:, u * PACK + j, b * P : (b + 1) * P],
+                        rhs=ident[:],
+                        start=(j == 0),
+                        stop=False,
+                        is_transpose=True,
+                    )
+
+        nc.scalar.dma_start(vs_pool[ROW:P, :], vs[ROW:P, :])
+        nc.sync.dma_start(voffs_t[:], voffs)
+
+        ks_g = sb.tile([P, N], U8, name="ks_g", align_bytes=64)
+        nc.vector.tensor_copy(ks_g[:], ks_pool[:].indirect(offs_t[:]))
+        nc.vector.memset(vsc_pool[:].bitcast(I32), 0)
+
+        v_scale_rows = v_scales.rearrange("u (g r) e -> r g u e", r=PACK)
+        for r in range(PACK):
+            nc.sync.dma_start(
+                vsc_pool[r:P:32, :].bitcast(I32).rearrange("g (u e) -> g u e", u=POOL_PAGES),
+                v_scale_rows[r].bitcast(I32),
+            )
+        nc.sync.dma_start(
+            vw_pool[:].rearrange("p (u e) -> p u e", u=POOL_PAGES),
+            v_words.rearrange("u p e r -> p u (e r)").bitcast(I32),
+        )
+
+        kw_g = sb.tile([P, N], U32, name="kw_g", align_bytes=64)
+        for u in range(PAGES):
+            nc.vector.tensor_copy(kw_g[:, u * PAGE : (u + 1) * PAGE], kw_pool[:].bitcast(U32).indirect(page_list(u)))
+
+        neg_tanh = sb.tile([P, BLOCKS * PAGES, PAGE], F32, name="neg_tanh")
+        for b in range(BLOCKS):
+            queries = slice(b * P, (b + 1) * P)
+            for u in range(PAGES):
+                unit = b * PAGES + u
+                score_bank = bank(6 + unit % 2, [P, PAGE])
+                for j in range(PACK):
+                    slots = slice(u * PAGE + j * P, u * PAGE + (j + 1) * P)
+                    nc.tensor.matmul_mx(
+                        out=score_bank[:, j * P : (j + 1) * P],
+                        lhsT=kw_g[:, slots].bitcast(FP8X4),
+                        lhsT_scale=ks_g[:, slots],
+                        rhs=qw[:, queries].bitcast(FP8X4),
+                        rhs_scale=qs[:, queries],
+                        start=True,
+                        stop=True,
+                    )
+                nc.scalar.activation(neg_tanh[:, unit, :], score_bank[:], ACT.Tanh, scale=-1.0 / CAP)
+                for j in range(PACK):
+                    nc.tensor.matmul(
+                        capped_banks[b][u][:, j * P : (j + 1) * P],
+                        lhsT=neg_tanh[:, unit, j * P : (j + 1) * P],
+                        rhs=ident[:],
+                        start=False,
+                        stop=(j == PACK - 1),
+                        is_transpose=True,
+                    )
+
+        vs_g = sb.tile([P, N], F32, name="vs_g")
+        nc.vector.tensor_copy(vs_g[:], vs_pool[:].indirect(offs_t[:]))
+
+        depth = sb.tile([P, BLOCKS * PAGES, PAGE], F32, name="depth")
+        least = [sb.tile([P, PAGES], F32, name="least%d" % b) for b in range(BLOCKS)]
+        doubled = [sb.tile([P, PAGES], F32, name="doubled%d" % b) for b in range(BLOCKS)]
+        shift = [sb.tile([P, 1], F32, name="shift%d" % b) for b in range(BLOCKS)]
+        sums = [sb.tile([P, PAGES], F32, name="sums%d" % b) for b in range(BLOCKS)]
+        total = [sb.tile([P, 1], F32, name="total%d" % b) for b in range(BLOCKS)]
+        inverse = [sb.tile([P, 1], F32, name="inverse%d" % b) for b in range(BLOCKS)]
+        probs = sb.tile([P, BLOCKS * PAGES, PAGE], F32, name="probs")
+        vs_cols = sb.tile([P, PAGES, PACK], F32, name="vs_cols")
+        vw_g = sb.tile([P, PAGES * DV], U32, name="vw_g", align_bytes=64)
+        vsc_g = sb.tile([P, PAGES * DV], U8, name="vsc_g", align_bytes=64)
+        w = sb.tile([P, BLOCKS * PAGES, PAGE], BF16, name="w", align_bytes=64)
+        w_codes = sb.tile([P, BLOCKS * PAGES, P], U32, name="w_codes", align_bytes=64)
+        w_scales = sb.tile([P, BLOCKS * PAGES, P], U8, name="w_scales", align_bytes=64)
+
+        def row_shift(b):
+            for u in range(PAGES):
+                nc.vector.tensor_scalar(
+                    out=depth[:, b * PAGES + u, :].rearrange("p (t m) -> p t m", t=PACK),
+                    in0=capped_banks[b][u][:].rearrange("p (m t) -> p t m", t=PACK),
+                    scalar1=-MASKED / CAP,
+                    scalar2=None,
+                    op0=ALU.min,
+                    op1=ALU.min,
+                    accum_out=least[b][:, u : u + 1],
+                )
+            nc.vector.tensor_scalar(
+                out=doubled[b][:], in0=least[b][:], scalar1=CAP, scalar2=None, op0=ALU.mult, op1=ALU.min,
+                accum_out=shift[b][:],
+            )
+
+        def exponentials(b):
+            for u in range(PAGES):
+                unit = b * PAGES + u
+                nc.scalar.activation(
+                    probs[:, unit, :], depth[:, unit, :], ACT.Exp, bias=shift[b][:], scale=-CAP,
+                    accum_out=sums[b][:, u : u + 1],
+                )
+
+        def weigh(b, u):
+            unit = b * PAGES + u
+            turned = bank(unit, [P, PACK, P])
+            for t in range(PACK):
+                nc.tensor.transpose(turned[:, t, :], probs[:, unit, t * P : (t + 1) * P], ident[:])
+            nc.vector.tensor_tensor(
+                w[:, unit, :].rearrange("p (q t) -> p q t", t=PACK),
+                turned[:].rearrange("p t q -> p q t"),
+                vs_cols[:, u : u + 1, :].to_broadcast([P, P, PACK]),
+                ALU.mult,
+            )
+
+        def quantize(unit):
+            nc.vector.quantize_mx(out=w_codes[:, unit, :].bitcast(FP8X4), scales=w_scales[:, unit, :], in_=w[:, unit, :])
+
+        def finish(b):
+            y_bank = bank(6 + b, [P, DV])
+            for u in range(PAGES):
+                columns = slice(u * DV, (u + 1) * DV)
+                nc.tensor.matmul_mx(
+                    out=y_bank[:],
+                    lhsT=w_codes[:, b * PAGES + u, :].bitcast(FP8X4),
+                    lhsT_scale=w_scales[:, b * PAGES + u, :],
+                    rhs=vw_g[:, columns].bitcast(FP8X4),
+                    rhs_scale=vsc_g[:, columns],
+                    start=(u == 0),
+                    stop=(u == PAGES - 1),
+                )
+            y = sb.tile([P, DV], F32, name="y%d" % b)
+            nc.scalar.activation(y[:], y_bank[:], ACT.Copy, scale=inverse[b][:])
+            nc.sync.dma_start(out[0, b * P : (b + 1) * P, :], y[:])
+
+        def invert_sum(b):
+            nc.vector.tensor_reduce(total[b][:], sums[b][:], AXIS.X, ALU.add)
+            nc.vector.reciprocal(inverse[b][:], total[b][:])
+
+        row_shift(0)
+        for u in range(PAGES):
+            vs_bank = bank(u, [P, PACK, P])
+            page = vs_g[:, u * PAGE : (u + 1) * PAGE].rearrange("p (m t) -> p t m", t=PACK)
+            for t in range(PACK):
+                nc.tensor.transpose(vs_bank[:, t, :], page[:, t, :], ident[:])
+            nc.scalar.activation(vs_cols[:, u, :], vs_bank[:, :, ROW], ACT.Copy)
+        exponentials(0)
+        row_shift(1)
+        exponentials(1)
+        nc.vector.tensor_copy(vsc_g[:], vsc_pool[:].indirect(voffs_t[:]))
+        weigh(0, 0)
+        weigh(0, 1)
+        quantize(0)
+        weigh(0, 2)
+        quantize(1)
+        invert_sum(0)
+        nc.vector.tensor_copy(vw_g[:], vw_pool[:].bitcast(U32).indirect(voffs_t[:]))
+        quantize(2)
+        finish(0)
+        weigh(1, 0)
+        weigh(1, 1)
+        quantize(3)
+        weigh(1, 2)
+        quantize(4)
+        invert_sum(1)
+        quantize(5)
+        finish(1)

@@ -46,11 +46,10 @@ def tile_attend_pkv8q_soft_draft_cap_kernel(
 
         offs_t = sb.tile([P, N // 16], U16, name="offs_t")
         voffs_t = sb.tile([P, PAGES * DV // 16], U16, name="voffs_t")
-        pos_pool = sb.tile([P, T], F32, name="pos_pool")
+        pos_pool = sb.tile([P, T], F32, name="pos_pool", tag="shared")
         vs_pool = sb.tile([P, T], F32, name="vs_pool")
         kw_pool = sb.tile([P, T], I32, name="kw_pool")
         ks_pool = sb.tile([P, T], U8, name="ks_pool")
-        vw_pool = sb.tile([P, POOL_PAGES * DV], I32, name="vw_pool")
         vsc_pool = sb.tile([P, POOL_PAGES * DV], U8, name="vsc_pool")
         qw = sb.tile([P, NQ], I32, name="qw", align_bytes=64)
         qs = sb.tile([P, NQ], U8, name="qs", align_bytes=64)
@@ -59,24 +58,26 @@ def tile_attend_pkv8q_soft_draft_cap_kernel(
         warm_in = sb.tile([P, 1], F32, name="warm_in")
         warm_out = sb.tile([P, 1], F32, name="warm_out")
 
-        nc.vector.memset(ks_pool[:].bitcast(I32), 0)
+        nc.gpsimd.memset(qs[:].bitcast(I32), 0)
         nc.vector.memset(warm_in[:], 0.0)
-        nc.vector.memset(qs[:].bitcast(I32), 0)
+        nc.vector.memset(ks_pool[:].bitcast(I32), 0)
         nc.scalar.activation(warm_out[:], warm_in[:], ACT.Exp)
         make_identity(nc, ident[:])
 
+        q_scale_rows = q_scales[0, 0].rearrange("(g r) q -> r g q", r=PACK)
+        k_scale_rows = k_scales[0].rearrange("(g r) t -> r g t", r=PACK)
         nc.sync.dma_start(offs_t[:], offs)
         nc.sync.dma_start(pos_pool[ROW:P, :], pos[ROW:P, :])
         nc.sync.dma_start(qpos_cols[:], qpos[0].rearrange("(p c) o -> p (c o)", c=BLOCKS))
-        k_scale_rows = k_scales[0].rearrange("(g r) t -> r g t", r=PACK)
-        for r in range(PACK):
-            nc.sync.dma_start(ks_pool[r:P:32, :].bitcast(I32), k_scale_rows[r].bitcast(I32))
+        nc.sync.dma_start(vs_pool[ROW:P, :], vs[ROW:P, :])
+        nc.sync.dma_start(voffs_t[:], voffs)
+        nc.sync.dma_start(qw[:], q_words[0, 0].rearrange("p q r -> p (q r)").bitcast(I32))
+        nc.sync.dma_start(qs[0:P:32, :].bitcast(I32), q_scale_rows[0].bitcast(I32))
         nc.sync.dma_start(kw_pool[:], k_words[0].rearrange("p t r -> p (t r)").bitcast(I32))
-
-        nc.scalar.dma_start(qw[:], q_words[0, 0].rearrange("p q r -> p (q r)").bitcast(I32))
-        q_scale_rows = q_scales[0, 0].rearrange("(g r) q -> r g q", r=PACK)
+        for r in range(1, PACK):
+            nc.sync.dma_start(qs[r:P:32, :].bitcast(I32), q_scale_rows[r].bitcast(I32))
         for r in range(PACK):
-            nc.scalar.dma_start(qs[r:P:32, :].bitcast(I32), q_scale_rows[r].bitcast(I32))
+            nc.scalar.dma_start(ks_pool[r:P:32, :].bitcast(I32), k_scale_rows[r].bitcast(I32))
 
         nc.vector.memset(pos_pool[0:ROW, :], 0.0)
         nc.vector.memset(vs_pool[0:ROW, 0:64], 0.0)
@@ -117,9 +118,6 @@ def tile_attend_pkv8q_soft_draft_cap_kernel(
                         is_transpose=True,
                     )
 
-        nc.scalar.dma_start(vs_pool[ROW:P, :], vs[ROW:P, :])
-        nc.sync.dma_start(voffs_t[:], voffs)
-
         ks_g = sb.tile([P, N], U8, name="ks_g", align_bytes=64)
         nc.vector.tensor_copy(ks_g[:], ks_pool[:].indirect(offs_t[:]))
         nc.vector.memset(vsc_pool[:].bitcast(I32), 0)
@@ -130,6 +128,7 @@ def tile_attend_pkv8q_soft_draft_cap_kernel(
                 vsc_pool[r:P:32, :].bitcast(I32).rearrange("g (u e) -> g u e", u=POOL_PAGES),
                 v_scale_rows[r].bitcast(I32),
             )
+        vw_pool = sb.tile([P, POOL_PAGES * DV], I32, name="vw_pool", tag="shared")
         nc.sync.dma_start(
             vw_pool[:].rearrange("p (u e) -> p u e", u=POOL_PAGES),
             v_words.rearrange("u p e r -> p u (e r)").bitcast(I32),
@@ -178,12 +177,16 @@ def tile_attend_pkv8q_soft_draft_cap_kernel(
         total = [sb.tile([P, 1], F32, name="total%d" % b) for b in range(BLOCKS)]
         inverse = [sb.tile([P, 1], F32, name="inverse%d" % b) for b in range(BLOCKS)]
         probs = sb.tile([P, BLOCKS * PAGES, PAGE], F32, name="probs")
-        vs_cols = sb.tile([P, PAGES, PACK], F32, name="vs_cols")
+        vs_cols = [sb.tile([P, 1, PACK], F32, name="vs_cols%d" % u) for u in range(PAGES)]
         vw_g = sb.tile([P, PAGES * DV], U32, name="vw_g", align_bytes=64)
         vsc_g = sb.tile([P, PAGES * DV], U8, name="vsc_g", align_bytes=64)
         w = sb.tile([P, BLOCKS * PAGES, PAGE], BF16, name="w", align_bytes=64)
         w_codes = sb.tile([P, BLOCKS * PAGES, P], U32, name="w_codes", align_bytes=64)
         w_scales = sb.tile([P, BLOCKS * PAGES, P], U8, name="w_scales", align_bytes=64)
+
+        for u in range(PAGES):
+            row = vs_g[ROW:P, u * PAGE : (u + 1) * PAGE].rearrange("o (m t) -> o m t", t=PACK)
+            nc.sync.dma_start(vs_cols[u][:, 0, :], row)
 
         def row_shift(b):
             for u in range(PAGES):
@@ -217,7 +220,7 @@ def tile_attend_pkv8q_soft_draft_cap_kernel(
             nc.vector.tensor_tensor(
                 w[:, unit, :].rearrange("p (q t) -> p q t", t=PACK),
                 turned[:].rearrange("p t q -> p q t"),
-                vs_cols[:, u : u + 1, :].to_broadcast([P, P, PACK]),
+                vs_cols[u][:].to_broadcast([P, P, PACK]),
                 ALU.mult,
             )
 
@@ -246,12 +249,6 @@ def tile_attend_pkv8q_soft_draft_cap_kernel(
             nc.vector.reciprocal(inverse[b][:], total[b][:])
 
         row_shift(0)
-        for u in range(PAGES):
-            vs_bank = bank(u, [P, PACK, P])
-            page = vs_g[:, u * PAGE : (u + 1) * PAGE].rearrange("p (m t) -> p t m", t=PACK)
-            for t in range(PACK):
-                nc.tensor.transpose(vs_bank[:, t, :], page[:, t, :], ident[:])
-            nc.scalar.activation(vs_cols[:, u, :], vs_bank[:, :, ROW], ACT.Copy)
         exponentials(0)
         row_shift(1)
         exponentials(1)

@@ -49,8 +49,7 @@ def tile_attend_pkv8q_soft_draft_cap_kernel(
         pos_pool = sb.tile([P, T], F32, name="pos_pool", tag="shared")
         vs_pool = sb.tile([P, T], F32, name="vs_pool")
         kw_pool = sb.tile([P, T], I32, name="kw_pool")
-        ks_pool = sb.tile([P, T], U8, name="ks_pool")
-        vsc_pool = sb.tile([P, POOL_PAGES * DV], U8, name="vsc_pool")
+        ks_pool = sb.tile([P, T], U8, name="ks_pool", tag="second")
         qw = sb.tile([P, NQ], I32, name="qw", align_bytes=64)
         qs = sb.tile([P, NQ], U8, name="qs", align_bytes=64)
         qpos_cols = sb.tile([P, BLOCKS], F32, name="qpos_cols")
@@ -94,10 +93,14 @@ def tile_attend_pkv8q_soft_draft_cap_kernel(
         pos_g = sb.tile([P, N], F32, name="pos_g")
         pos_cols = sb.tile([P, PAGES * PACK], F32, name="pos_cols")
         late = sb.tile([P, PAGES * PACK, NQ], F32, name="late")
-        capped_banks = [[bank(b * PAGES + u, [P, PAGE]) for u in range(PAGES)] for b in range(BLOCKS)]
-        for u in range(PAGES):
+        neg_tanh = sb.tile([P, BLOCKS * PAGES, PAGE], F32, name="neg_tanh")
+        capped = {}
+
+        def gather_places(u):
             nc.vector.tensor_copy(pos_g[:, u * PAGE : (u + 1) * PAGE], pos_pool[:].indirect(page_list(u)))
-            pos_bank = bank(7 - u % 2, [P, PACK, P])
+
+        def mask_page(u, bank_index):
+            pos_bank = bank(bank_index, [P, PACK, P])
             for j in range(PACK):
                 first = u * PAGE + j * P
                 nc.tensor.transpose(pos_bank[:, j, :], pos_g[:, first : first + P], ident[:])
@@ -107,20 +110,63 @@ def tile_attend_pkv8q_soft_draft_cap_kernel(
                 nc.scalar.activation(
                     late[:, chunk, :], qpos_rows[:], ACT.Relu, bias=pos_cols[:, chunk : chunk + 1], scale=-STEEP
                 )
-            for b in range(BLOCKS):
-                for j in range(PACK):
-                    nc.tensor.matmul(
-                        capped_banks[b][u][:, j * P : (j + 1) * P],
-                        lhsT=late[:, u * PACK + j, b * P : (b + 1) * P],
-                        rhs=ident[:],
-                        start=(j == 0),
-                        stop=False,
-                        is_transpose=True,
-                    )
+
+        def add_turned(unit, source):
+            opens = unit not in capped
+            if opens:
+                capped[unit] = bank(unit, [P, PAGE])
+            for j in range(PACK):
+                nc.tensor.matmul(
+                    capped[unit][:, j * P : (j + 1) * P],
+                    lhsT=source(j),
+                    rhs=ident[:],
+                    start=(opens and j == 0),
+                    stop=(not opens and j == PACK - 1),
+                    is_transpose=True,
+                )
+
+        def add_mask(unit):
+            b, u = divmod(unit, PAGES)
+            add_turned(unit, lambda j: late[:, u * PACK + j, b * P : (b + 1) * P])
+
+        def add_tanh(unit):
+            add_turned(unit, lambda j: neg_tanh[:, unit, j * P : (j + 1) * P])
+
+        def score(unit, bank_index):
+            b, u = divmod(unit, PAGES)
+            queries = slice(b * P, (b + 1) * P)
+            score_bank = bank(bank_index, [P, PAGE])
+            for j in range(PACK):
+                slots = slice(u * PAGE + j * P, u * PAGE + (j + 1) * P)
+                nc.tensor.matmul_mx(
+                    out=score_bank[:, j * P : (j + 1) * P],
+                    lhsT=kw_g[:, slots].bitcast(FP8X4),
+                    lhsT_scale=ks_g[:, slots],
+                    rhs=qw[:, queries].bitcast(FP8X4),
+                    rhs_scale=qs[:, queries],
+                    start=True,
+                    stop=True,
+                )
+            nc.scalar.activation(neg_tanh[:, unit, :], score_bank[:], ACT.Tanh, scale=-1.0 / CAP)
+
+        for u in range(2):
+            gather_places(u)
+            mask_page(u, 7 - 2 * u)
+            add_mask(u)
+            add_mask(PAGES + u)
+        gather_places(2)
+        mask_page(2, 7)
+        add_mask(2)
+        vw_pool = sb.tile([P, POOL_PAGES * DV], I32, name="vw_pool", tag="shared")
+        nc.sync.dma_start(
+            vw_pool[:].rearrange("p (u e) -> p u e", u=POOL_PAGES),
+            v_words.rearrange("u p e r -> p u (e r)").bitcast(I32),
+        )
 
         ks_g = sb.tile([P, N], U8, name="ks_g", align_bytes=64)
         nc.vector.tensor_copy(ks_g[:], ks_pool[:].indirect(offs_t[:]))
-        nc.vector.memset(vsc_pool[:].bitcast(I32), 0)
+        vsc_pool = sb.tile([P, POOL_PAGES * DV], U8, name="vsc_pool", tag="second")
+        nc.gpsimd.memset(vsc_pool[:].bitcast(I32), 0)
 
         v_scale_rows = v_scales.rearrange("u (g r) e -> r g u e", r=PACK)
         for r in range(PACK):
@@ -128,43 +174,24 @@ def tile_attend_pkv8q_soft_draft_cap_kernel(
                 vsc_pool[r:P:32, :].bitcast(I32).rearrange("g (u e) -> g u e", u=POOL_PAGES),
                 v_scale_rows[r].bitcast(I32),
             )
-        vw_pool = sb.tile([P, POOL_PAGES * DV], I32, name="vw_pool", tag="shared")
-        nc.sync.dma_start(
-            vw_pool[:].rearrange("p (u e) -> p u e", u=POOL_PAGES),
-            v_words.rearrange("u p e r -> p u (e r)").bitcast(I32),
-        )
 
         kw_g = sb.tile([P, N], U32, name="kw_g", align_bytes=64)
         for u in range(PAGES):
             nc.vector.tensor_copy(kw_g[:, u * PAGE : (u + 1) * PAGE], kw_pool[:].bitcast(U32).indirect(page_list(u)))
 
-        neg_tanh = sb.tile([P, BLOCKS * PAGES, PAGE], F32, name="neg_tanh")
-        for b in range(BLOCKS):
-            queries = slice(b * P, (b + 1) * P)
-            for u in range(PAGES):
-                unit = b * PAGES + u
-                score_bank = bank(6 + unit % 2, [P, PAGE])
-                for j in range(PACK):
-                    slots = slice(u * PAGE + j * P, u * PAGE + (j + 1) * P)
-                    nc.tensor.matmul_mx(
-                        out=score_bank[:, j * P : (j + 1) * P],
-                        lhsT=kw_g[:, slots].bitcast(FP8X4),
-                        lhsT_scale=ks_g[:, slots],
-                        rhs=qw[:, queries].bitcast(FP8X4),
-                        rhs_scale=qs[:, queries],
-                        start=True,
-                        stop=True,
-                    )
-                nc.scalar.activation(neg_tanh[:, unit, :], score_bank[:], ACT.Tanh, scale=-1.0 / CAP)
-                for j in range(PACK):
-                    nc.tensor.matmul(
-                        capped_banks[b][u][:, j * P : (j + 1) * P],
-                        lhsT=neg_tanh[:, unit, j * P : (j + 1) * P],
-                        rhs=ident[:],
-                        start=False,
-                        stop=(j == PACK - 1),
-                        is_transpose=True,
-                    )
+        score(0, 6)
+        score(1, 7)
+        score(2, 5)
+        add_tanh(0)
+        score(3, 6)
+        add_tanh(1)
+        score(4, 7)
+        add_tanh(2)
+        score(5, 6)
+        add_mask(5)
+        add_tanh(3)
+        add_tanh(4)
+        add_tanh(5)
 
         vs_g = sb.tile([P, N], F32, name="vs_g")
         nc.vector.tensor_copy(vs_g[:], vs_pool[:].indirect(offs_t[:]))
@@ -188,17 +215,18 @@ def tile_attend_pkv8q_soft_draft_cap_kernel(
             row = vs_g[ROW:P, u * PAGE : (u + 1) * PAGE].rearrange("o (m t) -> o m t", t=PACK)
             nc.sync.dma_start(vs_cols[u][:, 0, :], row)
 
+        def clamp(b, u):
+            nc.vector.tensor_scalar(
+                out=depth[:, b * PAGES + u, :].rearrange("p (t c i) -> p c t i", t=PACK, i=PACK),
+                in0=capped[b * PAGES + u][:].rearrange("p (c i t) -> p c t i", t=PACK, i=PACK),
+                scalar1=-MASKED / CAP,
+                scalar2=None,
+                op0=ALU.min,
+                op1=ALU.min,
+                accum_out=least[b][:, u : u + 1],
+            )
+
         def row_shift(b):
-            for u in range(PAGES):
-                nc.vector.tensor_scalar(
-                    out=depth[:, b * PAGES + u, :].rearrange("p (t m) -> p t m", t=PACK),
-                    in0=capped_banks[b][u][:].rearrange("p (m t) -> p t m", t=PACK),
-                    scalar1=-MASKED / CAP,
-                    scalar2=None,
-                    op0=ALU.min,
-                    op1=ALU.min,
-                    accum_out=least[b][:, u : u + 1],
-                )
             nc.vector.tensor_scalar(
                 out=doubled[b][:], in0=least[b][:], scalar1=CAP, scalar2=None, op0=ALU.mult, op1=ALU.min,
                 accum_out=shift[b][:],
@@ -212,11 +240,26 @@ def tile_attend_pkv8q_soft_draft_cap_kernel(
                     accum_out=sums[b][:, u : u + 1],
                 )
 
-        def weigh(b, u):
-            unit = b * PAGES + u
+        def turn(unit):
             turned = bank(unit, [P, PACK, P])
             for t in range(PACK):
                 nc.tensor.transpose(turned[:, t, :], probs[:, unit, t * P : (t + 1) * P], ident[:])
+            return turned
+
+        def weigh_on_scalar(b, u):
+            unit = b * PAGES + u
+            turned = turn(unit)
+            planes = sb.tile([P, PACK, P], BF16, name="planes%d" % unit)
+            for t in range(PACK):
+                nc.scalar.activation(planes[:, t, :], turned[:, t, :], ACT.Copy, scale=vs_cols[u][:, 0, t : t + 1])
+            nc.scalar.copy(
+                w[:, unit, :].rearrange("p (c i t) -> p c t i", t=PACK, i=PACK),
+                planes[:].rearrange("p t (c i) -> p c t i", i=PACK),
+            )
+
+        def weigh(b, u):
+            unit = b * PAGES + u
+            turned = turn(unit)
             nc.vector.tensor_tensor(
                 w[:, unit, :].rearrange("p (q t) -> p q t", t=PACK),
                 turned[:].rearrange("p t q -> p q t"),
@@ -227,9 +270,9 @@ def tile_attend_pkv8q_soft_draft_cap_kernel(
         def quantize(unit):
             nc.vector.quantize_mx(out=w_codes[:, unit, :].bitcast(FP8X4), scales=w_scales[:, unit, :], in_=w[:, unit, :])
 
-        def finish(b):
+        def finish(b, pages):
             y_bank = bank(6 + b, [P, DV])
-            for u in range(PAGES):
+            for u in pages:
                 columns = slice(u * DV, (u + 1) * DV)
                 nc.tensor.matmul_mx(
                     out=y_bank[:],
@@ -237,8 +280,8 @@ def tile_attend_pkv8q_soft_draft_cap_kernel(
                     lhsT_scale=w_scales[:, b * PAGES + u, :],
                     rhs=vw_g[:, columns].bitcast(FP8X4),
                     rhs_scale=vsc_g[:, columns],
-                    start=(u == 0),
-                    stop=(u == PAGES - 1),
+                    start=(u == pages[0]),
+                    stop=(u == pages[-1]),
                 )
             y = sb.tile([P, DV], F32, name="y%d" % b)
             nc.scalar.activation(y[:], y_bank[:], ACT.Copy, scale=inverse[b][:])
@@ -248,8 +291,15 @@ def tile_attend_pkv8q_soft_draft_cap_kernel(
             nc.vector.tensor_reduce(total[b][:], sums[b][:], AXIS.X, ALU.add)
             nc.vector.reciprocal(inverse[b][:], total[b][:])
 
+        clamp(0, 0)
+        clamp(0, 1)
+        clamp(0, 2)
         row_shift(0)
         exponentials(0)
+        nc.vector.tensor_copy(vw_g[:], vw_pool[:].bitcast(U32).indirect(voffs_t[:]))
+        clamp(1, 0)
+        clamp(1, 1)
+        clamp(1, 2)
         row_shift(1)
         exponentials(1)
         nc.vector.tensor_copy(vsc_g[:], vsc_pool[:].indirect(voffs_t[:]))
@@ -258,15 +308,14 @@ def tile_attend_pkv8q_soft_draft_cap_kernel(
         quantize(0)
         weigh(0, 2)
         quantize(1)
-        invert_sum(0)
-        nc.vector.tensor_copy(vw_g[:], vw_pool[:].bitcast(U32).indirect(voffs_t[:]))
-        quantize(2)
-        finish(0)
         weigh(1, 0)
-        weigh(1, 1)
-        quantize(3)
+        weigh_on_scalar(1, 1)
+        quantize(2)
+        invert_sum(0)
+        finish(0, [0, 1, 2])
         weigh(1, 2)
-        quantize(4)
         invert_sum(1)
+        quantize(3)
+        quantize(4)
         quantize(5)
-        finish(1)
+        finish(1, [0, 1, 2])

@@ -50,37 +50,36 @@ def tile_attend_pkv8q_soft_draft_cap_kernel(
         vs_pool = sb.tile([P, T], F32, name="vs_pool")
         kw_pool = sb.tile([P, T], I32, name="kw_pool")
         ks_pool = sb.tile([P, T], U8, name="ks_pool", tag="second")
-        qw = sb.tile([P, NQ], I32, name="qw", align_bytes=64)
         qs = sb.tile([P, NQ], U8, name="qs", align_bytes=64)
-        qpos_cols = sb.tile([P, BLOCKS], F32, name="qpos_cols")
         ident = sb.tile([P, P], F32, name="ident")
-        warm_in = sb.tile([P, 1], F32, name="warm_in")
+        warm_in = sb.tile([P, 1], F32, name="warm_in", tag="warm_in", align_bytes=64)
         warm_out = sb.tile([P, 1], F32, name="warm_out")
 
-        nc.gpsimd.memset(qs[:].bitcast(I32), 0)
+        make_identity(nc, ident[:])
         nc.vector.memset(warm_in[:], 0.0)
         nc.vector.memset(ks_pool[:].bitcast(I32), 0)
         nc.scalar.activation(warm_out[:], warm_in[:], ACT.Exp)
-        make_identity(nc, ident[:])
+        nc.vector.memset(pos_pool[0:ROW, :], 0.0)
+        nc.vector.memset(vs_pool[:, 0:64], 0.0)
+        nc.vector.memset(qs[:].bitcast(I32), 0)
+        nc.gpsimd.memset(vs_pool[0:ROW, 56:T], 0.0)
 
-        q_scale_rows = q_scales[0, 0].rearrange("(g r) q -> r g q", r=PACK)
+        qw = sb.tile([P, NQ], I32, name="qw", tag="warm_in", align_bytes=64)
+        qpos_cols = sb.tile([P, BLOCKS], F32, name="qpos_cols", tag="qpos_cols")
         k_scale_rows = k_scales[0].rearrange("(g r) t -> r g t", r=PACK)
         nc.sync.dma_start(offs_t[:], offs)
         nc.sync.dma_start(pos_pool[ROW:P, :], pos[ROW:P, :])
         nc.sync.dma_start(qpos_cols[:], qpos[0].rearrange("(p c) o -> p (c o)", c=BLOCKS))
-        nc.sync.dma_start(vs_pool[ROW:P, :], vs[ROW:P, :])
         nc.sync.dma_start(voffs_t[:], voffs)
-        nc.sync.dma_start(qw[:], q_words[0, 0].rearrange("p q r -> p (q r)").bitcast(I32))
-        nc.sync.dma_start(qs[0:P:32, :].bitcast(I32), q_scale_rows[0].bitcast(I32))
         nc.sync.dma_start(kw_pool[:], k_words[0].rearrange("p t r -> p (t r)").bitcast(I32))
-        for r in range(1, PACK):
-            nc.sync.dma_start(qs[r:P:32, :].bitcast(I32), q_scale_rows[r].bitcast(I32))
         for r in range(PACK):
             nc.scalar.dma_start(ks_pool[r:P:32, :].bitcast(I32), k_scale_rows[r].bitcast(I32))
-
-        nc.vector.memset(pos_pool[0:ROW, :], 0.0)
-        nc.vector.memset(vs_pool[0:ROW, 0:64], 0.0)
-        nc.gpsimd.memset(vs_pool[0:ROW, 56:T], 0.0)
+        nc.sync.dma_start(qw[:], q_words[0, 0].rearrange("p q r -> p (q r)").bitcast(I32))
+        nc.sync.dma_start(vs_pool[ROW:P, :], vs[ROW:P, :])
+        for g in range(PACK):
+            nc.sync.dma_start(
+                qs[32 * g : 32 * g + PACK, :].bitcast(I32), q_scales[0, 0, PACK * g : PACK * (g + 1), :].bitcast(I32)
+            )
 
         qpos_bank = bank(6, [P, BLOCKS, P])
         for c in range(BLOCKS):

@@ -28,6 +28,7 @@ BLOCKS = NQ // P
 LIST_COLS = PAGE // 16
 ROW = P - 1
 STEEP = 2.0**60
+UNIT_BANK = (0, 2, 6, 1, 3, 7)
 
 
 def tile_attend_pkv8q_soft_draft_cap_kernel(
@@ -81,7 +82,7 @@ def tile_attend_pkv8q_soft_draft_cap_kernel(
                 qs[32 * g : 32 * g + PACK, :].bitcast(I32), q_scales[0, 0, PACK * g : PACK * (g + 1), :].bitcast(I32)
             )
 
-        qpos_bank = bank(6, [P, BLOCKS, P])
+        qpos_bank = bank(4, [P, BLOCKS, P])
         for c in range(BLOCKS):
             nc.tensor.transpose(qpos_bank[:, c, :], qpos_cols[:, c : c + 1].to_broadcast([P, P]), ident[:])
         qpos_rows = sb.tile([P, NQ], F32, name="qpos_rows")
@@ -113,7 +114,7 @@ def tile_attend_pkv8q_soft_draft_cap_kernel(
         def add_turned(unit, source):
             opens = unit not in capped
             if opens:
-                capped[unit] = bank(unit, [P, PAGE])
+                capped[unit] = bank(UNIT_BANK[unit], [P, PAGE])
             for j in range(PACK):
                 nc.tensor.matmul(
                     capped[unit][:, j * P : (j + 1) * P],
@@ -150,12 +151,11 @@ def tile_attend_pkv8q_soft_draft_cap_kernel(
 
         for u in range(2):
             gather_places(u)
-            mask_page(u, 7 - 2 * u)
+            mask_page(u, 5 + u)
             add_mask(u)
             add_mask(PAGES + u)
         gather_places(2)
         mask_page(2, 7)
-        add_mask(2)
         vw_pool = sb.tile([P, POOL_PAGES * DV], I32, name="vw_pool", tag="shared")
         nc.sync.dma_start(
             vw_pool[:].rearrange("p (u e) -> p u e", u=POOL_PAGES),
@@ -178,17 +178,18 @@ def tile_attend_pkv8q_soft_draft_cap_kernel(
         for u in range(PAGES):
             nc.vector.tensor_copy(kw_g[:, u * PAGE : (u + 1) * PAGE], kw_pool[:].bitcast(U32).indirect(page_list(u)))
 
-        score(0, 6)
-        score(1, 7)
-        score(2, 5)
+        score(0, 4)
+        score(3, 5)
+        score(1, 6)
+        score(2, 7)
         add_tanh(0)
-        score(3, 6)
+        score(4, 4)
         add_tanh(1)
-        score(4, 7)
+        add_mask(2)
+        score(5, 5)
         add_tanh(2)
-        score(5, 6)
-        add_mask(5)
         add_tanh(3)
+        add_mask(5)
         add_tanh(4)
         add_tanh(5)
 
@@ -199,9 +200,9 @@ def tile_attend_pkv8q_soft_draft_cap_kernel(
         least = [sb.tile([P, PAGES], F32, name="least%d" % b) for b in range(BLOCKS)]
         doubled = [sb.tile([P, PAGES], F32, name="doubled%d" % b) for b in range(BLOCKS)]
         shift = [sb.tile([P, 1], F32, name="shift%d" % b) for b in range(BLOCKS)]
-        sums = [sb.tile([P, PAGES], F32, name="sums%d" % b) for b in range(BLOCKS)]
-        total = [sb.tile([P, 1], F32, name="total%d" % b) for b in range(BLOCKS)]
-        inverse = [sb.tile([P, 1], F32, name="inverse%d" % b) for b in range(BLOCKS)]
+        sums = sb.tile([P, BLOCKS, PAGES], F32, name="sums")
+        total = sb.tile([P, BLOCKS], F32, name="total")
+        inverse = sb.tile([P, BLOCKS], F32, name="inverse")
         probs = sb.tile([P, BLOCKS * PAGES, PAGE], F32, name="probs")
         vs_cols = [sb.tile([P, 1, PACK], F32, name="vs_cols%d" % u) for u in range(PAGES)]
         vw_g = sb.tile([P, PAGES * DV], U32, name="vw_g", align_bytes=64)
@@ -236,11 +237,11 @@ def tile_attend_pkv8q_soft_draft_cap_kernel(
                 unit = b * PAGES + u
                 nc.scalar.activation(
                     probs[:, unit, :], depth[:, unit, :], ACT.Exp, bias=shift[b][:], scale=-CAP,
-                    accum_out=sums[b][:, u : u + 1],
+                    accum_out=sums[:, b, u : u + 1],
                 )
 
         def turn(unit):
-            turned = bank(unit, [P, PACK, P])
+            turned = bank(UNIT_BANK[unit], [P, PACK, P])
             for t in range(PACK):
                 nc.tensor.transpose(turned[:, t, :], probs[:, unit, t * P : (t + 1) * P], ident[:])
             return turned
@@ -270,7 +271,7 @@ def tile_attend_pkv8q_soft_draft_cap_kernel(
             nc.vector.quantize_mx(out=w_codes[:, unit, :].bitcast(FP8X4), scales=w_scales[:, unit, :], in_=w[:, unit, :])
 
         def finish(b, pages):
-            y_bank = bank(6 + b, [P, DV])
+            y_bank = bank(4 + b, [P, DV])
             for u in pages:
                 columns = slice(u * DV, (u + 1) * DV)
                 nc.tensor.matmul_mx(
@@ -283,12 +284,8 @@ def tile_attend_pkv8q_soft_draft_cap_kernel(
                     stop=(u == pages[-1]),
                 )
             y = sb.tile([P, DV], F32, name="y%d" % b)
-            nc.scalar.activation(y[:], y_bank[:], ACT.Copy, scale=inverse[b][:])
+            nc.scalar.activation(y[:], y_bank[:], ACT.Copy, scale=inverse[:, b : b + 1])
             nc.sync.dma_start(out[0, b * P : (b + 1) * P, :], y[:])
-
-        def invert_sum(b):
-            nc.vector.tensor_reduce(total[b][:], sums[b][:], AXIS.X, ALU.add)
-            nc.vector.reciprocal(inverse[b][:], total[b][:])
 
         clamp(0, 0)
         clamp(0, 1)
@@ -310,11 +307,11 @@ def tile_attend_pkv8q_soft_draft_cap_kernel(
         weigh(1, 0)
         weigh_on_scalar(1, 1)
         quantize(2)
-        invert_sum(0)
-        finish(0, [0, 1, 2])
-        weigh(1, 2)
-        invert_sum(1)
+        nc.vector.tensor_reduce(total[:], sums[:], AXIS.X, ALU.add)
         quantize(3)
+        weigh(1, 2)
+        nc.vector.reciprocal(inverse[:], total[:])
         quantize(4)
         quantize(5)
+        finish(0, [0, 1, 2])
         finish(1, [0, 1, 2])

@@ -53,19 +53,15 @@ def tile_attend_pkv8q_soft_draft_cap_kernel(
         ks_pool = sb.tile([P, T], U8, name="ks_pool", tag="second")
         qs = sb.tile([P, NQ], U8, name="qs", align_bytes=64)
         ident = sb.tile([P, P], F32, name="ident")
-        warm_in = sb.tile([P, 1], F32, name="warm_in", tag="warm_in", align_bytes=64)
-        warm_out = sb.tile([P, 1], F32, name="warm_out")
 
         make_identity(nc, ident[:])
-        nc.vector.memset(warm_in[:], 0.0)
         nc.vector.memset(ks_pool[:].bitcast(I32), 0)
-        nc.scalar.activation(warm_out[:], warm_in[:], ACT.Exp)
         nc.vector.memset(pos_pool[0:ROW, :], 0.0)
         nc.vector.memset(vs_pool[:, 0:64], 0.0)
         nc.vector.memset(qs[:].bitcast(I32), 0)
         nc.gpsimd.memset(vs_pool[0:ROW, 56:T], 0.0)
 
-        qw = sb.tile([P, NQ], I32, name="qw", tag="warm_in", align_bytes=64)
+        qw = sb.tile([P, NQ], I32, name="qw", align_bytes=64)
         qpos_cols = sb.tile([P, BLOCKS], F32, name="qpos_cols", tag="qpos_cols")
         k_scale_rows = k_scales[0].rearrange("(g r) t -> r g t", r=PACK)
         nc.sync.dma_start(offs_t[:], offs)

@@ -28,7 +28,7 @@ BLOCKS = NQ // P
 LIST_COLS = PAGE // 16
 ROW = P - 1
 STEEP = 2.0**60
-UNIT_BANK = (0, 2, 6, 1, 3, 7)
+UNIT_BANK = (0, 2, 5, 1, 6, 7)
 
 
 def tile_attend_pkv8q_soft_draft_cap_kernel(
@@ -89,7 +89,7 @@ def tile_attend_pkv8q_soft_draft_cap_kernel(
         pos_g = sb.tile([P, N], F32, name="pos_g")
         pos_cols = sb.tile([P, PAGES * PACK], F32, name="pos_cols")
         late = sb.tile([P, PAGES * PACK, NQ], F32, name="late")
-        neg_tanh = sb.tile([P, BLOCKS * PAGES, PAGE], F32, name="neg_tanh")
+        neg_tanh = [sb.tile([P, PAGE], F32, name="neg_tanh%d" % n, tag="page%d" % n) for n in range(BLOCKS * PAGES)]
         capped = {}
 
         def gather_places(u):
@@ -126,7 +126,7 @@ def tile_attend_pkv8q_soft_draft_cap_kernel(
             add_turned(unit, lambda j: late[:, u * PACK + j, b * P : (b + 1) * P])
 
         def add_tanh(unit):
-            add_turned(unit, lambda j: neg_tanh[:, unit, j * P : (j + 1) * P])
+            add_turned(unit, lambda j: neg_tanh[unit][:, j * P : (j + 1) * P])
 
         def score(unit, bank_index):
             b, u = divmod(unit, PAGES)
@@ -143,15 +143,14 @@ def tile_attend_pkv8q_soft_draft_cap_kernel(
                     start=True,
                     stop=True,
                 )
-            nc.scalar.activation(neg_tanh[:, unit, :], score_bank[:], ACT.Tanh, scale=-1.0 / CAP)
+            nc.scalar.activation(neg_tanh[unit][:], score_bank[:], ACT.Tanh, scale=-1.0 / CAP)
 
-        for u in range(2):
+        for u in range(PAGES):
             gather_places(u)
             mask_page(u, 5 + u)
-            add_mask(u)
-            add_mask(PAGES + u)
-        gather_places(2)
-        mask_page(2, 7)
+        add_mask(0)
+        add_mask(3)
+        add_mask(1)
         vw_pool = sb.tile([P, POOL_PAGES * DV], I32, name="vw_pool", tag="shared")
         nc.sync.dma_start(
             vw_pool[:].rearrange("p (u e) -> p u e", u=POOL_PAGES),
@@ -174,42 +173,48 @@ def tile_attend_pkv8q_soft_draft_cap_kernel(
         for u in range(PAGES):
             nc.vector.tensor_copy(kw_g[:, u * PAGE : (u + 1) * PAGE], kw_pool[:].bitcast(U32).indirect(page_list(u)))
 
+        vs_cols = [sb.tile([P, 1, PACK], F32, name="vs_cols%d" % u) for u in range(PAGES)]
+
+        def scale_columns(u, vs_g):
+            nc.sync.dma_start(vs_cols[u][:, 0, :], vs_g[ROW:P, :].rearrange("o (m t) -> o m t", t=PACK))
+
+        vs_first = sb.tile([P, PAGE], F32, name="vs_first")
+        nc.vector.tensor_copy(vs_first[:], vs_pool[:].indirect(page_list(0)))
+        scale_columns(0, vs_first)
+
         score(0, 4)
         score(3, 5)
         score(1, 6)
         score(2, 7)
+        score(4, 3)
+        score(5, 4)
         add_tanh(0)
-        score(4, 4)
-        add_tanh(1)
-        add_mask(2)
-        score(5, 5)
-        add_tanh(2)
         add_tanh(3)
-        add_mask(5)
+        add_mask(2)
+        add_tanh(1)
+        add_tanh(2)
+        add_mask(4)
         add_tanh(4)
+        add_mask(5)
         add_tanh(5)
+        for u, freed in ((1, 0), (2, 3)):
+            vs_g = sb.tile([P, PAGE], F32, name="vs_g%d" % u, tag="page%d" % freed)
+            nc.scalar.activation(vs_g[:], vs_pool[:].indirect(page_list(u)), ACT.Copy)
+            scale_columns(u, vs_g)
 
-        vs_g = sb.tile([P, N], F32, name="vs_g")
-        nc.vector.tensor_copy(vs_g[:], vs_pool[:].indirect(offs_t[:]))
-
-        depth = sb.tile([P, BLOCKS * PAGES, PAGE], F32, name="depth")
-        least = [sb.tile([P, PAGES], F32, name="least%d" % b) for b in range(BLOCKS)]
+        vw_g = sb.tile([P, PAGES * DV], U32, name="vw_g", align_bytes=64)
+        nc.vector.tensor_copy(vw_g[:], vw_pool[:].bitcast(U32).indirect(voffs_t[:]))
+        depth = sb.tile([P, BLOCKS * PAGES, PAGE], F32, name="depth", tag="shared")
+        least = [sb.tile([P, PAGES], F32, name="least%d" % b, tag="least%d" % b, align_bytes=64) for b in range(BLOCKS)]
         doubled = [sb.tile([P, PAGES], F32, name="doubled%d" % b) for b in range(BLOCKS)]
         shift = [sb.tile([P, 1], F32, name="shift%d" % b) for b in range(BLOCKS)]
         sums = sb.tile([P, BLOCKS, PAGES], F32, name="sums")
         total = sb.tile([P, BLOCKS], F32, name="total")
         inverse = sb.tile([P, BLOCKS], F32, name="inverse")
         probs = sb.tile([P, BLOCKS * PAGES, PAGE], F32, name="probs")
-        vs_cols = [sb.tile([P, 1, PACK], F32, name="vs_cols%d" % u) for u in range(PAGES)]
-        vw_g = sb.tile([P, PAGES * DV], U32, name="vw_g", align_bytes=64)
-        vsc_g = sb.tile([P, PAGES * DV], U8, name="vsc_g", align_bytes=64)
         w = sb.tile([P, BLOCKS * PAGES, PAGE], BF16, name="w", align_bytes=64)
         w_codes = sb.tile([P, BLOCKS * PAGES, P], U32, name="w_codes", align_bytes=64)
         w_scales = sb.tile([P, BLOCKS * PAGES, P], U8, name="w_scales", align_bytes=64)
-
-        for u in range(PAGES):
-            row = vs_g[ROW:P, u * PAGE : (u + 1) * PAGE].rearrange("o (m t) -> o m t", t=PACK)
-            nc.sync.dma_start(vs_cols[u][:, 0, :], row)
 
         def clamp(b, u):
             nc.vector.tensor_scalar(
@@ -267,7 +272,7 @@ def tile_attend_pkv8q_soft_draft_cap_kernel(
             nc.vector.quantize_mx(out=w_codes[:, unit, :].bitcast(FP8X4), scales=w_scales[:, unit, :], in_=w[:, unit, :])
 
         def finish(b, pages):
-            y_bank = bank(4 + b, [P, DV])
+            y_bank = bank(3 + b, [P, DV])
             for u in pages:
                 columns = slice(u * DV, (u + 1) * DV)
                 nc.tensor.matmul_mx(
@@ -284,16 +289,16 @@ def tile_attend_pkv8q_soft_draft_cap_kernel(
             nc.sync.dma_start(out[0, b * P : (b + 1) * P, :], y[:])
 
         clamp(0, 0)
+        clamp(1, 0)
         clamp(0, 1)
         clamp(0, 2)
         row_shift(0)
         exponentials(0)
-        nc.vector.tensor_copy(vw_g[:], vw_pool[:].bitcast(U32).indirect(voffs_t[:]))
-        clamp(1, 0)
         clamp(1, 1)
         clamp(1, 2)
         row_shift(1)
         exponentials(1)
+        vsc_g = sb.tile([P, PAGES * DV], U8, name="vsc_g", tag="least1", align_bytes=64)
         nc.vector.tensor_copy(vsc_g[:], vsc_pool[:].indirect(voffs_t[:]))
         weigh(0, 0)
         weigh(0, 1)

@@ -29,6 +29,8 @@ LIST_COLS = PAGE // 16
 ROW = P - 1
 STEEP = 2.0**60
 UNIT_BANK = (0, 2, 5, 1, 6, 7)
+SCORE_BANK = (4, 5, 6, 7, 3, 4)
+EARLY_MASKS = (0, 3, 1)
 
 
 def tile_attend_pkv8q_soft_draft_cap_kernel(
@@ -148,9 +150,8 @@ def tile_attend_pkv8q_soft_draft_cap_kernel(
         for u in range(PAGES):
             gather_places(u)
             mask_page(u, 5 + u)
-        add_mask(0)
-        add_mask(3)
-        add_mask(1)
+        for unit in EARLY_MASKS:
+            add_mask(unit)
         vw_pool = sb.tile([P, POOL_PAGES * DV], I32, name="vw_pool", tag="shared")
         nc.sync.dma_start(
             vw_pool[:].rearrange("p (u e) -> p u e", u=POOL_PAGES),
@@ -182,22 +183,13 @@ def tile_attend_pkv8q_soft_draft_cap_kernel(
         nc.vector.tensor_copy(vs_first[:], vs_pool[:].indirect(page_list(0)))
         scale_columns(0, vs_first)
 
-        score(0, 4)
-        score(3, 5)
-        score(1, 6)
-        score(2, 7)
-        score(4, 3)
-        score(5, 4)
-        add_tanh(0)
-        add_tanh(3)
-        add_mask(2)
-        add_tanh(1)
-        add_tanh(2)
-        add_mask(4)
-        add_tanh(4)
-        add_mask(5)
-        add_tanh(5)
-        for u, freed in ((1, 0), (2, 3)):
+        for unit, bank_index in enumerate(SCORE_BANK):
+            score(unit, bank_index)
+        for unit in range(BLOCKS * PAGES):
+            if unit not in EARLY_MASKS:
+                add_mask(unit)
+            add_tanh(unit)
+        for u, freed in ((1, 0), (2, 1)):
             vs_g = sb.tile([P, PAGE], F32, name="vs_g%d" % u, tag="page%d" % freed)
             nc.scalar.activation(vs_g[:], vs_pool[:].indirect(page_list(u)), ACT.Copy)
             scale_columns(u, vs_g)
@@ -218,8 +210,8 @@ def tile_attend_pkv8q_soft_draft_cap_kernel(
 
         def clamp(b, u):
             nc.vector.tensor_scalar(
-                out=depth[:, b * PAGES + u, :].rearrange("p (t c i) -> p c t i", t=PACK, i=PACK),
-                in0=capped[b * PAGES + u][:].rearrange("p (c i t) -> p c t i", t=PACK, i=PACK),
+                out=depth[:, b * PAGES + u, :].rearrange("p (t s) -> p t s", t=PACK),
+                in0=capped[b * PAGES + u][:].rearrange("p (s t) -> p t s", t=PACK),
                 scalar1=-MASKED / CAP,
                 scalar2=None,
                 op0=ALU.min,
@@ -288,16 +280,11 @@ def tile_attend_pkv8q_soft_draft_cap_kernel(
             nc.scalar.activation(y[:], y_bank[:], ACT.Copy, scale=inverse[:, b : b + 1])
             nc.sync.dma_start(out[0, b * P : (b + 1) * P, :], y[:])
 
-        clamp(0, 0)
-        clamp(1, 0)
-        clamp(0, 1)
-        clamp(0, 2)
-        row_shift(0)
-        exponentials(0)
-        clamp(1, 1)
-        clamp(1, 2)
-        row_shift(1)
-        exponentials(1)
+        for b in range(BLOCKS):
+            for u in range(PAGES):
+                clamp(b, u)
+            row_shift(b)
+            exponentials(b)
         vsc_g = sb.tile([P, PAGES * DV], U8, name="vsc_g", tag="least1", align_bytes=64)
         nc.vector.tensor_copy(vsc_g[:], vsc_pool[:].indirect(voffs_t[:]))
         weigh(0, 0)

@@ -28,6 +28,7 @@ BLOCKS = NQ // P
 LIST_COLS = PAGE // 16
 ROW = P - 1
 STEEP = 2.0**60
+HALF = PACK // 2
 UNIT_BANK = (0, 2, 5, 1, 6, 7)
 SCORE_BANK = (4, 5, 6, 7, 3, 4)
 EARLY_MASKS = (0, 3, 1)
@@ -49,7 +50,7 @@ def tile_attend_pkv8q_soft_draft_cap_kernel(
 
         offs_t = sb.tile([P, N // 16], U16, name="offs_t")
         voffs_t = sb.tile([P, PAGES * DV // 16], U16, name="voffs_t")
-        pos_pool = sb.tile([P, T], F32, name="pos_pool", tag="shared")
+        pos_pool = sb.tile([P, T], F32, name="pos_pool")
         vs_pool = sb.tile([P, T], F32, name="vs_pool")
         kw_pool = sb.tile([P, T], I32, name="kw_pool")
         ks_pool = sb.tile([P, T], U8, name="ks_pool", tag="second")
@@ -58,9 +59,9 @@ def tile_attend_pkv8q_soft_draft_cap_kernel(
 
         make_identity(nc, ident[:])
         nc.vector.memset(ks_pool[:].bitcast(I32), 0)
-        nc.vector.memset(pos_pool[0:ROW, :], 0.0)
-        nc.vector.memset(vs_pool[:, 0:64], 0.0)
         nc.vector.memset(qs[:].bitcast(I32), 0)
+        nc.vector.memset(pos_pool[0:ROW, :], 0.0)
+        nc.vector.memset(vs_pool[0:ROW, 0:64], 0.0)
         nc.gpsimd.memset(vs_pool[0:ROW, 56:T], 0.0)
 
         qw = sb.tile([P, NQ], I32, name="qw", align_bytes=64)
@@ -69,16 +70,21 @@ def tile_attend_pkv8q_soft_draft_cap_kernel(
         nc.sync.dma_start(offs_t[:], offs)
         nc.sync.dma_start(pos_pool[ROW:P, :], pos[ROW:P, :])
         nc.sync.dma_start(qpos_cols[:], qpos[0].rearrange("(p c) o -> p (c o)", c=BLOCKS))
-        nc.sync.dma_start(voffs_t[:], voffs)
         nc.sync.dma_start(kw_pool[:], k_words[0].rearrange("p t r -> p (t r)").bitcast(I32))
         for r in range(PACK):
             nc.scalar.dma_start(ks_pool[r:P:32, :].bitcast(I32), k_scale_rows[r].bitcast(I32))
         nc.sync.dma_start(qw[:], q_words[0, 0].rearrange("p q r -> p (q r)").bitcast(I32))
-        nc.sync.dma_start(vs_pool[ROW:P, :], vs[ROW:P, :])
         for g in range(PACK):
             nc.sync.dma_start(
                 qs[32 * g : 32 * g + PACK, :].bitcast(I32), q_scales[0, 0, PACK * g : PACK * (g + 1), :].bitcast(I32)
             )
+        nc.sync.dma_start(vs_pool[ROW:P, :], vs[ROW:P, :])
+        vw_pool = sb.tile([P, POOL_PAGES * DV], I32, name="vw_pool", tag="values")
+        nc.sync.dma_start(
+            vw_pool[:].rearrange("p (u e) -> p u e", u=POOL_PAGES),
+            v_words.rearrange("u p e r -> p u (e r)").bitcast(I32),
+        )
+        nc.sync.dma_start(voffs_t[:], voffs)
 
         qpos_bank = bank(4, [P, BLOCKS, P])
         for c in range(BLOCKS):
@@ -94,17 +100,16 @@ def tile_attend_pkv8q_soft_draft_cap_kernel(
         neg_tanh = [sb.tile([P, PAGE], F32, name="neg_tanh%d" % n, tag="page%d" % n) for n in range(BLOCKS * PAGES)]
         capped = {}
 
-        def gather_places(u):
-            nc.vector.tensor_copy(pos_g[:, u * PAGE : (u + 1) * PAGE], pos_pool[:].indirect(page_list(u)))
+        def gather_places(first, count):
+            entries = offs_t[:, first * P // 16 : (first + count) * P // 16]
+            return pos_g[:, first * P : (first + count) * P], pos_pool[:].indirect(entries)
 
-        def mask_page(u, bank_index):
-            pos_bank = bank(bank_index, [P, PACK, P])
-            for j in range(PACK):
-                first = u * PAGE + j * P
-                nc.tensor.transpose(pos_bank[:, j, :], pos_g[:, first : first + P], ident[:])
-            nc.scalar.activation(pos_cols[:, u * PACK : (u + 1) * PACK], pos_bank[:, :, ROW], ACT.Copy, scale=STEEP)
-            for j in range(PACK):
-                chunk = u * PACK + j
+        def mask_chunks(first, count, bank_index):
+            pos_bank = bank(bank_index, [P, count, P])
+            for j in range(count):
+                nc.tensor.transpose(pos_bank[:, j, :], pos_g[:, (first + j) * P : (first + j + 1) * P], ident[:])
+            nc.scalar.activation(pos_cols[:, first : first + count], pos_bank[:, :, ROW], ACT.Copy, scale=STEEP)
+            for chunk in range(first, first + count):
                 nc.scalar.activation(
                     late[:, chunk, :], qpos_rows[:], ACT.Relu, bias=pos_cols[:, chunk : chunk + 1], scale=-STEEP
                 )
@@ -147,16 +152,16 @@ def tile_attend_pkv8q_soft_draft_cap_kernel(
                 )
             nc.scalar.activation(neg_tanh[unit][:], score_bank[:], ACT.Tanh, scale=-1.0 / CAP)
 
-        for u in range(PAGES):
-            gather_places(u)
-            mask_page(u, 5 + u)
+        nc.vector.tensor_copy(*gather_places(0, HALF))
+        nc.vector.tensor_copy(*gather_places(HALF, HALF))
+        nc.vector.tensor_copy(*gather_places(PACK, PACK))
+        nc.scalar.activation(*gather_places(2 * PACK, PACK), ACT.Copy)
+        mask_chunks(0, HALF, 3)
+        mask_chunks(HALF, HALF, 5)
+        mask_chunks(PACK, PACK, 6)
+        mask_chunks(2 * PACK, PACK, 7)
         for unit in EARLY_MASKS:
             add_mask(unit)
-        vw_pool = sb.tile([P, POOL_PAGES * DV], I32, name="vw_pool", tag="shared")
-        nc.sync.dma_start(
-            vw_pool[:].rearrange("p (u e) -> p u e", u=POOL_PAGES),
-            v_words.rearrange("u p e r -> p u (e r)").bitcast(I32),
-        )
 
         ks_g = sb.tile([P, N], U8, name="ks_g", align_bytes=64)
         nc.vector.tensor_copy(ks_g[:], ks_pool[:].indirect(offs_t[:]))
@@ -196,7 +201,7 @@ def tile_attend_pkv8q_soft_draft_cap_kernel(
 
         vw_g = sb.tile([P, PAGES * DV], U32, name="vw_g", align_bytes=64)
         nc.vector.tensor_copy(vw_g[:], vw_pool[:].bitcast(U32).indirect(voffs_t[:]))
-        depth = sb.tile([P, BLOCKS * PAGES, PAGE], F32, name="depth", tag="shared")
+        depth = sb.tile([P, BLOCKS * PAGES, PAGE], F32, name="depth", tag="values")
         least = [sb.tile([P, PAGES], F32, name="least%d" % b, tag="least%d" % b, align_bytes=64) for b in range(BLOCKS)]
         doubled = [sb.tile([P, PAGES], F32, name="doubled%d" % b) for b in range(BLOCKS)]
         shift = [sb.tile([P, 1], F32, name="shift%d" % b) for b in range(BLOCKS)]
@@ -263,22 +268,34 @@ def tile_attend_pkv8q_soft_draft_cap_kernel(
         def quantize(unit):
             nc.vector.quantize_mx(out=w_codes[:, unit, :].bitcast(FP8X4), scales=w_scales[:, unit, :], in_=w[:, unit, :])
 
-        def finish(b, pages):
-            y_bank = bank(3 + b, [P, DV])
-            for u in pages:
-                columns = slice(u * DV, (u + 1) * DV)
+        def multiply(b, features, bank_index):
+            y_bank = bank(bank_index, [P, features.stop - features.start])
+            for u in range(PAGES):
+                columns = slice(u * DV + features.start, u * DV + features.stop)
                 nc.tensor.matmul_mx(
                     out=y_bank[:],
                     lhsT=w_codes[:, b * PAGES + u, :].bitcast(FP8X4),
                     lhsT_scale=w_scales[:, b * PAGES + u, :],
                     rhs=vw_g[:, columns].bitcast(FP8X4),
                     rhs_scale=vsc_g[:, columns],
-                    start=(u == pages[0]),
-                    stop=(u == pages[-1]),
+                    start=(u == 0),
+                    stop=(u == PAGES - 1),
                 )
-            y = sb.tile([P, DV], F32, name="y%d" % b)
+            return y_bank
+
+        def finish_on_scalar(b, features, bank_index):
+            y_bank = multiply(b, features, bank_index)
+            y = sb.tile([P, features.stop - features.start], F32, name="y%d" % bank_index)
             nc.scalar.activation(y[:], y_bank[:], ACT.Copy, scale=inverse[:, b : b + 1])
-            nc.sync.dma_start(out[0, b * P : (b + 1) * P, :], y[:])
+            nc.sync.dma_start(out[0, b * P : (b + 1) * P, features], y[:])
+
+        def finish_on_vector(b, features, bank_index):
+            y_bank = multiply(b, features, bank_index)
+            y = sb.tile([P, features.stop - features.start], F32, name="y%d" % bank_index)
+            nc.vector.tensor_scalar(
+                out=y[:], in0=y_bank[:], scalar1=inverse[:, b : b + 1], scalar2=None, op0=ALU.mult
+            )
+            nc.scalar.dma_start(out[0, b * P : (b + 1) * P, features], y[:])
 
         for b in range(BLOCKS):
             for u in range(PAGES):
@@ -301,5 +318,6 @@ def tile_attend_pkv8q_soft_draft_cap_kernel(
         nc.vector.reciprocal(inverse[:], total[:])
         quantize(4)
         quantize(5)
-        finish(0, [0, 1, 2])
-        finish(1, [0, 1, 2])
+        finish_on_scalar(0, slice(0, DV), 3)
+        finish_on_scalar(1, slice(0, DV // 2), 4)
+        finish_on_vector(1, slice(DV // 2, DV), UNIT_BANK[0])

@@ -29,9 +29,12 @@ LIST_COLS = PAGE // 16
 ROW = P - 1
 STEEP = 2.0**60
 HALF = PACK // 2
+KEYS_AHEAD = 1280
 UNIT_BANK = (0, 2, 5, 1, 6, 7)
 SCORE_BANK = (4, 5, 6, 7, 3, 4)
 EARLY_MASKS = (0, 3, 1)
+SCORE_ORDER = (0, 3, 1, 4, 2, 5)
+PAGE_ORDER = ((0, 1, 2), (1, 0, 2))
 
 
 def tile_attend_pkv8q_soft_draft_cap_kernel(
@@ -70,15 +73,17 @@ def tile_attend_pkv8q_soft_draft_cap_kernel(
         nc.sync.dma_start(offs_t[:], offs)
         nc.sync.dma_start(pos_pool[ROW:P, :], pos[ROW:P, :])
         nc.sync.dma_start(qpos_cols[:], qpos[0].rearrange("(p c) o -> p (c o)", c=BLOCKS))
-        nc.sync.dma_start(kw_pool[:], k_words[0].rearrange("p t r -> p (t r)").bitcast(I32))
+        key_words = k_words[0].rearrange("p t r -> p (t r)").bitcast(I32)
+        nc.sync.dma_start(kw_pool[:, 0:KEYS_AHEAD], key_words[:, 0:KEYS_AHEAD])
         for r in range(PACK):
-            nc.scalar.dma_start(ks_pool[r:P:32, :].bitcast(I32), k_scale_rows[r].bitcast(I32))
+            nc.sync.dma_start(ks_pool[r:P:32, :].bitcast(I32), k_scale_rows[r].bitcast(I32))
+        nc.sync.dma_start(kw_pool[:, KEYS_AHEAD:T], key_words[:, KEYS_AHEAD:T])
         nc.sync.dma_start(qw[:], q_words[0, 0].rearrange("p q r -> p (q r)").bitcast(I32))
+        nc.sync.dma_start(vs_pool[ROW:P, :], vs[ROW:P, :])
         for g in range(PACK):
             nc.sync.dma_start(
                 qs[32 * g : 32 * g + PACK, :].bitcast(I32), q_scales[0, 0, PACK * g : PACK * (g + 1), :].bitcast(I32)
             )
-        nc.sync.dma_start(vs_pool[ROW:P, :], vs[ROW:P, :])
         vw_pool = sb.tile([P, POOL_PAGES * DV], I32, name="vw_pool", tag="values")
         nc.sync.dma_start(
             vw_pool[:].rearrange("p (u e) -> p u e", u=POOL_PAGES),
@@ -188,7 +193,7 @@ def tile_attend_pkv8q_soft_draft_cap_kernel(
         nc.vector.tensor_copy(vs_first[:], vs_pool[:].indirect(page_list(0)))
         scale_columns(0, vs_first)
 
-        for unit, bank_index in enumerate(SCORE_BANK):
+        for unit, bank_index in zip(SCORE_ORDER, SCORE_BANK):
             score(unit, bank_index)
         for unit in range(BLOCKS * PAGES):
             if unit not in EARLY_MASKS:
@@ -270,7 +275,8 @@ def tile_attend_pkv8q_soft_draft_cap_kernel(
 
         def multiply(b, features, bank_index):
             y_bank = bank(bank_index, [P, features.stop - features.start])
-            for u in range(PAGES):
+            pages = PAGE_ORDER[b]
+            for u in pages:
                 columns = slice(u * DV + features.start, u * DV + features.stop)
                 nc.tensor.matmul_mx(
                     out=y_bank[:],
@@ -278,8 +284,8 @@ def tile_attend_pkv8q_soft_draft_cap_kernel(
                     lhsT_scale=w_scales[:, b * PAGES + u, :],
                     rhs=vw_g[:, columns].bitcast(FP8X4),
                     rhs_scale=vsc_g[:, columns],
-                    start=(u == 0),
-                    stop=(u == PAGES - 1),
+                    start=(u == pages[0]),
+                    stop=(u == pages[-1]),
                 )
             return y_bank
 
@@ -288,14 +294,6 @@ def tile_attend_pkv8q_soft_draft_cap_kernel(
             y = sb.tile([P, features.stop - features.start], F32, name="y%d" % bank_index)
             nc.scalar.activation(y[:], y_bank[:], ACT.Copy, scale=inverse[:, b : b + 1])
             nc.sync.dma_start(out[0, b * P : (b + 1) * P, features], y[:])
-
-        def finish_on_vector(b, features, bank_index):
-            y_bank = multiply(b, features, bank_index)
-            y = sb.tile([P, features.stop - features.start], F32, name="y%d" % bank_index)
-            nc.vector.tensor_scalar(
-                out=y[:], in0=y_bank[:], scalar1=inverse[:, b : b + 1], scalar2=None, op0=ALU.mult
-            )
-            nc.scalar.dma_start(out[0, b * P : (b + 1) * P, features], y[:])
 
         for b in range(BLOCKS):
             for u in range(PAGES):
@@ -309,15 +307,14 @@ def tile_attend_pkv8q_soft_draft_cap_kernel(
         quantize(0)
         weigh(0, 2)
         quantize(1)
-        weigh(1, 0)
-        weigh_on_scalar(1, 1)
+        weigh_on_scalar(1, 0)
+        weigh(1, 1)
         quantize(2)
         nc.vector.tensor_reduce(total[:], sums[:], AXIS.X, ALU.add)
-        quantize(3)
+        quantize(4)
         weigh(1, 2)
         nc.vector.reciprocal(inverse[:], total[:])
-        quantize(4)
+        quantize(3)
         quantize(5)
         finish_on_scalar(0, slice(0, DV), 3)
-        finish_on_scalar(1, slice(0, DV // 2), 4)
-        finish_on_vector(1, slice(DV // 2, DV), UNIT_BANK[0])
+        finish_on_scalar(1, slice(0, DV), 4)

@@ -1,3 +1,4 @@
+import math
 from contextlib import ExitStack
 
 import concourse.mybir as mybir
@@ -6,7 +7,7 @@ from concourse.masks import make_identity
 N, T, D, DV, NQ = 1536, 4096, 512, 256, 256
 PAGE = 512
 CAP = 2.0
-MASKED = -30000.0
+UNSEEN = math.log(8.0)
 FLOPS = 2 * NQ * N * (D + DV)
 
 F32 = mybir.dt.float32
@@ -84,7 +85,7 @@ def tile_attend_pkv8q_soft_draft_cap_kernel(
             nc.sync.dma_start(
                 qs[32 * g : 32 * g + PACK, :].bitcast(I32), q_scales[0, 0, PACK * g : PACK * (g + 1), :].bitcast(I32)
             )
-        vw_pool = sb.tile([P, POOL_PAGES * DV], I32, name="vw_pool", tag="values")
+        vw_pool = sb.tile([P, POOL_PAGES * DV], I32, name="vw_pool", tag="values", align_bytes=64)
         nc.sync.dma_start(
             vw_pool[:].rearrange("p (u e) -> p u e", u=POOL_PAGES),
             v_words.rearrange("u p e r -> p u (e r)").bitcast(I32),
@@ -206,8 +207,8 @@ def tile_attend_pkv8q_soft_draft_cap_kernel(
 
         vw_g = sb.tile([P, PAGES * DV], U32, name="vw_g", align_bytes=64)
         nc.vector.tensor_copy(vw_g[:], vw_pool[:].bitcast(U32).indirect(voffs_t[:]))
-        depth = sb.tile([P, BLOCKS * PAGES, PAGE], F32, name="depth", tag="values")
-        least = [sb.tile([P, PAGES], F32, name="least%d" % b, tag="least%d" % b, align_bytes=64) for b in range(BLOCKS)]
+        least = sb.tile([P, BLOCKS, PAGES], F32, name="least", tag="values", align_bytes=64)
+        down = [sb.tile([P, 1], F32, name="down%d" % b) for b in range(BLOCKS)]
         doubled = [sb.tile([P, PAGES], F32, name="doubled%d" % b) for b in range(BLOCKS)]
         shift = [sb.tile([P, 1], F32, name="shift%d" % b) for b in range(BLOCKS)]
         sums = sb.tile([P, BLOCKS, PAGES], F32, name="sums")
@@ -218,29 +219,25 @@ def tile_attend_pkv8q_soft_draft_cap_kernel(
         w_codes = sb.tile([P, BLOCKS * PAGES, P], U32, name="w_codes", align_bytes=64)
         w_scales = sb.tile([P, BLOCKS * PAGES, P], U8, name="w_scales", align_bytes=64)
 
-        def clamp(b, u):
-            nc.vector.tensor_scalar(
-                out=depth[:, b * PAGES + u, :].rearrange("p (t s) -> p t s", t=PACK),
-                in0=capped[b * PAGES + u][:].rearrange("p (s t) -> p t s", t=PACK),
-                scalar1=-MASKED / CAP,
-                scalar2=None,
-                op0=ALU.min,
-                op1=ALU.min,
-                accum_out=least[b][:, u : u + 1],
-            )
+        def page_minimum(b, u):
+            nc.vector.tensor_reduce(least[:, b, u : u + 1], capped[b * PAGES + u][:], AXIS.X, ALU.min)
 
         def row_shift(b):
             nc.vector.tensor_scalar(
-                out=doubled[b][:], in0=least[b][:], scalar1=CAP, scalar2=None, op0=ALU.mult, op1=ALU.min,
+                out=doubled[b][:], in0=least[:, b, :], scalar1=CAP, scalar2=UNSEEN, op0=ALU.mult, op1=ALU.min,
                 accum_out=shift[b][:],
+            )
+            nc.gpsimd.tensor_scalar(
+                out=down[b][:], in0=shift[b][:], scalar1=(CAP + UNSEEN) / 2, scalar2=-CAP, op0=ALU.is_lt, op1=ALU.mult
             )
 
         def exponentials(b):
             for u in range(PAGES):
                 unit = b * PAGES + u
                 nc.scalar.activation(
-                    probs[:, unit, :], depth[:, unit, :], ACT.Exp, bias=shift[b][:], scale=-CAP,
-                    accum_out=sums[:, b, u : u + 1],
+                    probs[:, unit, :].rearrange("p (t s) -> p t s", t=PACK),
+                    capped[unit][:].rearrange("p (s t) -> p t s", t=PACK),
+                    ACT.Exp, bias=shift[b][:], scale=down[b][:], accum_out=sums[:, b, u : u + 1],
                 )
 
         def turn(unit):
@@ -297,10 +294,10 @@ def tile_attend_pkv8q_soft_draft_cap_kernel(
 
         for b in range(BLOCKS):
             for u in range(PAGES):
-                clamp(b, u)
+                page_minimum(b, u)
             row_shift(b)
             exponentials(b)
-        vsc_g = sb.tile([P, PAGES * DV], U8, name="vsc_g", tag="least1", align_bytes=64)
+        vsc_g = sb.tile([P, PAGES * DV], U8, name="vsc_g", tag="values", align_bytes=64)
         nc.vector.tensor_copy(vsc_g[:], vsc_pool[:].indirect(voffs_t[:]))
         weigh(0, 0)
         weigh(0, 1)

import math
from contextlib import ExitStack

import concourse.mybir as mybir
from concourse.masks import make_identity

N, T, D, DV, NQ = 1536, 4096, 512, 256, 256
PAGE = 512
CAP = 2.0
UNSEEN = math.log(8.0)
FLOPS = 2 * NQ * N * (D + DV)

F32 = mybir.dt.float32
BF16 = mybir.dt.bfloat16
I32 = mybir.dt.int32
U32 = mybir.dt.uint32
U16 = mybir.dt.uint16
U8 = mybir.dt.uint8
FP8X4 = mybir.dt.float8_e4m3fn_x4
ALU = mybir.AluOpType
ACT = mybir.ActivationFunctionType
AXIS = mybir.AxisListType

P = 128
PACK = 4
PAGES = N // PAGE
POOL_PAGES = T // PAGE
BLOCKS = NQ // P
LIST_COLS = PAGE // 16
ROW = P - 1
STEEP = 2.0**60
HALF = PACK // 2
KEYS_AHEAD = 1280
UNIT_BANK = (0, 2, 5, 1, 6, 7)
SCORE_BANK = (4, 5, 6, 7, 3, 4)
EARLY_MASKS = (0, 3, 1)
SCORE_ORDER = (0, 3, 1, 4, 2, 5)
PAGE_ORDER = ((0, 1, 2), (1, 0, 2))


def tile_attend_pkv8q_soft_draft_cap_kernel(
    tc, q_words, q_scales, k_words, k_scales, v_words, v_scales, vs, pos, qpos, offs, voffs, out
):
    nc = tc.nc
    with ExitStack() as ctx:
        sb = ctx.enter_context(tc.tile_pool(name="sb", bufs=1))
        psum = ctx.enter_context(tc.psum_pool(name="psum", bufs=1))

        def bank(index, shape):
            return psum.tile(shape, F32, name="bank%d" % index, tag="bank%d" % index)

        def page_list(u):
            return offs_t[:, u * LIST_COLS : (u + 1) * LIST_COLS]

        offs_t = sb.tile([P, N // 16], U16, name="offs_t")
        voffs_t = sb.tile([P, PAGES * DV // 16], U16, name="voffs_t")
        pos_pool = sb.tile([P, T], F32, name="pos_pool")
        vs_pool = sb.tile([P, T], F32, name="vs_pool")
        kw_pool = sb.tile([P, T], I32, name="kw_pool")
        ks_pool = sb.tile([P, T], U8, name="ks_pool", tag="second")
        qs = sb.tile([P, NQ], U8, name="qs", align_bytes=64)
        ident = sb.tile([P, P], F32, name="ident")

        make_identity(nc, ident[:])
        nc.vector.memset(ks_pool[:].bitcast(I32), 0)
        nc.vector.memset(qs[:].bitcast(I32), 0)
        nc.vector.memset(pos_pool[0:ROW, :], 0.0)
        nc.vector.memset(vs_pool[0:ROW, 0:64], 0.0)
        nc.gpsimd.memset(vs_pool[0:ROW, 56:T], 0.0)

        qw = sb.tile([P, NQ], I32, name="qw", align_bytes=64)
        qpos_cols = sb.tile([P, BLOCKS], F32, name="qpos_cols", tag="qpos_cols")
        k_scale_rows = k_scales[0].rearrange("(g r) t -> r g t", r=PACK)
        nc.sync.dma_start(offs_t[:], offs)
        nc.sync.dma_start(pos_pool[ROW:P, :], pos[ROW:P, :])
        nc.sync.dma_start(qpos_cols[:], qpos[0].rearrange("(p c) o -> p (c o)", c=BLOCKS))
        key_words = k_words[0].rearrange("p t r -> p (t r)").bitcast(I32)
        nc.sync.dma_start(kw_pool[:, 0:KEYS_AHEAD], key_words[:, 0:KEYS_AHEAD])
        for r in range(PACK):
            nc.sync.dma_start(ks_pool[r:P:32, :].bitcast(I32), k_scale_rows[r].bitcast(I32))
        nc.sync.dma_start(kw_pool[:, KEYS_AHEAD:T], key_words[:, KEYS_AHEAD:T])
        nc.sync.dma_start(qw[:], q_words[0, 0].rearrange("p q r -> p (q r)").bitcast(I32))
        nc.sync.dma_start(vs_pool[ROW:P, :], vs[ROW:P, :])
        for g in range(PACK):
            nc.sync.dma_start(
                qs[32 * g : 32 * g + PACK, :].bitcast(I32), q_scales[0, 0, PACK * g : PACK * (g + 1), :].bitcast(I32)
            )
        vw_pool = sb.tile([P, POOL_PAGES * DV], I32, name="vw_pool", tag="values", align_bytes=64)
        nc.sync.dma_start(
            vw_pool[:].rearrange("p (u e) -> p u e", u=POOL_PAGES),
            v_words.rearrange("u p e r -> p u (e r)").bitcast(I32),
        )
        nc.sync.dma_start(voffs_t[:], voffs)

        qpos_bank = bank(4, [P, BLOCKS, P])
        for c in range(BLOCKS):
            nc.tensor.transpose(qpos_bank[:, c, :], qpos_cols[:, c : c + 1].to_broadcast([P, P]), ident[:])
        qpos_rows = sb.tile([P, NQ], F32, name="qpos_rows")
        nc.scalar.activation(
            qpos_rows[:].rearrange("p (q c) -> p q c", c=BLOCKS), qpos_bank[:].rearrange("p c q -> p q c"), ACT.Copy
        )

        pos_g = sb.tile([P, N], F32, name="pos_g")
        pos_cols = sb.tile([P, PAGES * PACK], F32, name="pos_cols")
        late = sb.tile([P, PAGES * PACK, NQ], F32, name="late")
        neg_tanh = [sb.tile([P, PAGE], F32, name="neg_tanh%d" % n, tag="page%d" % n) for n in range(BLOCKS * PAGES)]
        capped = {}

        def gather_places(first, count):
            entries = offs_t[:, first * P // 16 : (first + count) * P // 16]
            return pos_g[:, first * P : (first + count) * P], pos_pool[:].indirect(entries)

        def mask_chunks(first, count, bank_index):
            pos_bank = bank(bank_index, [P, count, P])
            for j in range(count):
                nc.tensor.transpose(pos_bank[:, j, :], pos_g[:, (first + j) * P : (first + j + 1) * P], ident[:])
            nc.scalar.activation(pos_cols[:, first : first + count], pos_bank[:, :, ROW], ACT.Copy, scale=STEEP)
            for chunk in range(first, first + count):
                nc.scalar.activation(
                    late[:, chunk, :], qpos_rows[:], ACT.Relu, bias=pos_cols[:, chunk : chunk + 1], scale=-STEEP
                )

        def add_turned(unit, source):
            opens = unit not in capped
            if opens:
                capped[unit] = bank(UNIT_BANK[unit], [P, PAGE])
            for j in range(PACK):
                nc.tensor.matmul(
                    capped[unit][:, j * P : (j + 1) * P],
                    lhsT=source(j),
                    rhs=ident[:],
                    start=(opens and j == 0),
                    stop=(not opens and j == PACK - 1),
                    is_transpose=True,
                )

        def add_mask(unit):
            b, u = divmod(unit, PAGES)
            add_turned(unit, lambda j: late[:, u * PACK + j, b * P : (b + 1) * P])

        def add_tanh(unit):
            add_turned(unit, lambda j: neg_tanh[unit][:, j * P : (j + 1) * P])

        def score(unit, bank_index):
            b, u = divmod(unit, PAGES)
            queries = slice(b * P, (b + 1) * P)
            score_bank = bank(bank_index, [P, PAGE])
            for j in range(PACK):
                slots = slice(u * PAGE + j * P, u * PAGE + (j + 1) * P)
                nc.tensor.matmul_mx(
                    out=score_bank[:, j * P : (j + 1) * P],
                    lhsT=kw_g[:, slots].bitcast(FP8X4),
                    lhsT_scale=ks_g[:, slots],
                    rhs=qw[:, queries].bitcast(FP8X4),
                    rhs_scale=qs[:, queries],
                    start=True,
                    stop=True,
                )
            nc.scalar.activation(neg_tanh[unit][:], score_bank[:], ACT.Tanh, scale=-1.0 / CAP)

        nc.vector.tensor_copy(*gather_places(0, HALF))
        nc.vector.tensor_copy(*gather_places(HALF, HALF))
        nc.vector.tensor_copy(*gather_places(PACK, PACK))
        nc.scalar.activation(*gather_places(2 * PACK, PACK), ACT.Copy)
        mask_chunks(0, HALF, 3)
        mask_chunks(HALF, HALF, 5)
        mask_chunks(PACK, PACK, 6)
        mask_chunks(2 * PACK, PACK, 7)
        for unit in EARLY_MASKS:
            add_mask(unit)

        ks_g = sb.tile([P, N], U8, name="ks_g", align_bytes=64)
        nc.vector.tensor_copy(ks_g[:], ks_pool[:].indirect(offs_t[:]))
        vsc_pool = sb.tile([P, POOL_PAGES * DV], U8, name="vsc_pool", tag="second")
        nc.gpsimd.memset(vsc_pool[:].bitcast(I32), 0)

        v_scale_rows = v_scales.rearrange("u (g r) e -> r g u e", r=PACK)
        for r in range(PACK):
            nc.sync.dma_start(
                vsc_pool[r:P:32, :].bitcast(I32).rearrange("g (u e) -> g u e", u=POOL_PAGES),
                v_scale_rows[r].bitcast(I32),
            )

        kw_g = sb.tile([P, N], U32, name="kw_g", align_bytes=64)
        for u in range(PAGES):
            nc.vector.tensor_copy(kw_g[:, u * PAGE : (u + 1) * PAGE], kw_pool[:].bitcast(U32).indirect(page_list(u)))

        vs_cols = [sb.tile([P, 1, PACK], F32, name="vs_cols%d" % u) for u in range(PAGES)]

        def scale_columns(u, vs_g):
            nc.sync.dma_start(vs_cols[u][:, 0, :], vs_g[ROW:P, :].rearrange("o (m t) -> o m t", t=PACK))

        vs_first = sb.tile([P, PAGE], F32, name="vs_first")
        nc.vector.tensor_copy(vs_first[:], vs_pool[:].indirect(page_list(0)))
        scale_columns(0, vs_first)

        for unit, bank_index in zip(SCORE_ORDER, SCORE_BANK):
            score(unit, bank_index)
        for unit in range(BLOCKS * PAGES):
            if unit not in EARLY_MASKS:
                add_mask(unit)
            add_tanh(unit)
        for u, freed in ((1, 0), (2, 1)):
            vs_g = sb.tile([P, PAGE], F32, name="vs_g%d" % u, tag="page%d" % freed)
            nc.scalar.activation(vs_g[:], vs_pool[:].indirect(page_list(u)), ACT.Copy)
            scale_columns(u, vs_g)

        vw_g = sb.tile([P, PAGES * DV], U32, name="vw_g", align_bytes=64)
        nc.vector.tensor_copy(vw_g[:], vw_pool[:].bitcast(U32).indirect(voffs_t[:]))
        least = sb.tile([P, BLOCKS, PAGES], F32, name="least", tag="values", align_bytes=64)
        down = [sb.tile([P, 1], F32, name="down%d" % b) for b in range(BLOCKS)]
        doubled = [sb.tile([P, PAGES], F32, name="doubled%d" % b) for b in range(BLOCKS)]
        shift = [sb.tile([P, 1], F32, name="shift%d" % b) for b in range(BLOCKS)]
        sums = sb.tile([P, BLOCKS, PAGES], F32, name="sums")
        total = sb.tile([P, BLOCKS], F32, name="total")
        inverse = sb.tile([P, BLOCKS], F32, name="inverse")
        probs = sb.tile([P, BLOCKS * PAGES, PAGE], F32, name="probs")
        w = sb.tile([P, BLOCKS * PAGES, PAGE], BF16, name="w", align_bytes=64)
        w_codes = sb.tile([P, BLOCKS * PAGES, P], U32, name="w_codes", align_bytes=64)
        w_scales = sb.tile([P, BLOCKS * PAGES, P], U8, name="w_scales", align_bytes=64)

        def page_minimum(b, u):
            nc.vector.tensor_reduce(least[:, b, u : u + 1], capped[b * PAGES + u][:], AXIS.X, ALU.min)

        def row_shift(b):
            nc.vector.tensor_scalar(
                out=doubled[b][:], in0=least[:, b, :], scalar1=CAP, scalar2=UNSEEN, op0=ALU.mult, op1=ALU.min,
                accum_out=shift[b][:],
            )
            nc.gpsimd.tensor_scalar(
                out=down[b][:], in0=shift[b][:], scalar1=(CAP + UNSEEN) / 2, scalar2=-CAP, op0=ALU.is_lt, op1=ALU.mult
            )

        def exponentials(b):
            for u in range(PAGES):
                unit = b * PAGES + u
                nc.scalar.activation(
                    probs[:, unit, :].rearrange("p (t s) -> p t s", t=PACK),
                    capped[unit][:].rearrange("p (s t) -> p t s", t=PACK),
                    ACT.Exp, bias=shift[b][:], scale=down[b][:], accum_out=sums[:, b, u : u + 1],
                )

        def turn(unit):
            turned = bank(UNIT_BANK[unit], [P, PACK, P])
            for t in range(PACK):
                nc.tensor.transpose(turned[:, t, :], probs[:, unit, t * P : (t + 1) * P], ident[:])
            return turned

        def weigh_on_scalar(b, u):
            unit = b * PAGES + u
            turned = turn(unit)
            planes = sb.tile([P, PACK, P], BF16, name="planes%d" % unit)
            for t in range(PACK):
                nc.scalar.activation(planes[:, t, :], turned[:, t, :], ACT.Copy, scale=vs_cols[u][:, 0, t : t + 1])
            nc.scalar.copy(
                w[:, unit, :].rearrange("p (c i t) -> p c t i", t=PACK, i=PACK),
                planes[:].rearrange("p t (c i) -> p c t i", i=PACK),
            )

        def weigh(b, u):
            unit = b * PAGES + u
            turned = turn(unit)
            nc.vector.tensor_tensor(
                w[:, unit, :].rearrange("p (q t) -> p q t", t=PACK),
                turned[:].rearrange("p t q -> p q t"),
                vs_cols[u][:].to_broadcast([P, P, PACK]),
                ALU.mult,
            )

        def quantize(unit):
            nc.vector.quantize_mx(out=w_codes[:, unit, :].bitcast(FP8X4), scales=w_scales[:, unit, :], in_=w[:, unit, :])

        def multiply(b, features, bank_index):
            y_bank = bank(bank_index, [P, features.stop - features.start])
            pages = PAGE_ORDER[b]
            for u in pages:
                columns = slice(u * DV + features.start, u * DV + features.stop)
                nc.tensor.matmul_mx(
                    out=y_bank[:],
                    lhsT=w_codes[:, b * PAGES + u, :].bitcast(FP8X4),
                    lhsT_scale=w_scales[:, b * PAGES + u, :],
                    rhs=vw_g[:, columns].bitcast(FP8X4),
                    rhs_scale=vsc_g[:, columns],
                    start=(u == pages[0]),
                    stop=(u == pages[-1]),
                )
            return y_bank

        def finish_on_scalar(b, features, bank_index):
            y_bank = multiply(b, features, bank_index)
            y = sb.tile([P, features.stop - features.start], F32, name="y%d" % bank_index)
            nc.scalar.activation(y[:], y_bank[:], ACT.Copy, scale=inverse[:, b : b + 1])
            nc.sync.dma_start(out[0, b * P : (b + 1) * P, features], y[:])

        for b in range(BLOCKS):
            for u in range(PAGES):
                page_minimum(b, u)
            row_shift(b)
            exponentials(b)
        vsc_g = sb.tile([P, PAGES * DV], U8, name="vsc_g", tag="values", align_bytes=64)
        nc.vector.tensor_copy(vsc_g[:], vsc_pool[:].indirect(voffs_t[:]))
        weigh(0, 0)
        weigh(0, 1)
        quantize(0)
        weigh(0, 2)
        quantize(1)
        weigh_on_scalar(1, 0)
        weigh(1, 1)
        quantize(2)
        nc.vector.tensor_reduce(total[:], sums[:], AXIS.X, ALU.add)
        quantize(4)
        weigh(1, 2)
        nc.vector.reciprocal(inverse[:], total[:])
        quantize(3)
        quantize(5)
        finish_on_scalar(0, slice(0, DV), 3)
        finish_on_scalar(1, slice(0, DV), 4)
